import numpy as np
import ml_dtypes


def mxq(x, axis, fmt="e4m3"):
    dtype, down = {"e4m3": (ml_dtypes.float8_e4m3fn, 7), "e5m2": (ml_dtypes.float8_e5m2, 14)}[fmt]
    v = np.moveaxis(np.asarray(x, np.float32).astype(ml_dtypes.bfloat16).astype(np.float64), axis, -1)
    blocks = v.reshape(v.shape[:-1] + (-1, 32))
    amax = np.abs(blocks).max(-1, keepdims=True)
    byte = np.maximum(np.where(amax > 0, np.frexp(amax)[1] - 1 + 127, 0) - down, 1)
    scale = np.exp2(byte - 127.0)
    codes = (blocks / scale).astype(np.float32).astype(dtype).astype(np.float64)
    return np.moveaxis((codes * scale).reshape(v.shape), -1, axis)


WIDE = False


def mx_kscale(k):
    if not WIDE:
        return np.ones(k)
    levels = np.array([10, -10, 5, -5, 0])
    if k % 512:
        return np.exp2(np.random.permutation(np.resize(levels, k // 32))).repeat(32)
    a = np.empty((k // 512, 16))
    for p in range(k // 512):
        a[p, :8] = np.random.permutation(np.resize(levels, 8))
        for g in range(8):
            far = levels[np.abs(levels - a[p, g]) >= 10]
            a[p, g + 8] = far[np.random.randint(len(far))]
    return np.exp2(a.ravel()).repeat(32)


BF16 = ml_dtypes.bfloat16


def bf(x):
    return np.asarray(x, np.float32).astype(BF16)


def f64(x):
    return np.asarray(x).astype(np.float64)


E2M1 = np.array([0.0, 0.5, 1.0, 1.5, 2.0, 3.0, 4.0, 6.0, -0.0, -0.5, -1.0, -1.5, -2.0, -3.0, -4.0, -6.0])


def pack_weight(w, fmt):
    k, n = w.shape
    w = f64(bf(w)).reshape(k // 32, 32, n)
    amax = np.abs(w).max(1)
    if fmt == "e4m3":
        byte = np.frexp(amax)[1] - 1 + 127 - 7
    else:
        mant, ex = np.frexp(amax / 6.0)
        byte = np.where(mant > 0.5, ex, ex - 1) + 127
    byte = np.clip(np.where(amax > 0, byte, 1), 1, 254)
    scaled = (w * np.exp2(127.0 - byte)[:, None, :]).reshape(k, n).astype(np.float32)
    by_word = np.ascontiguousarray(scaled.reshape(k // 512, 128, 4, n).transpose(0, 1, 3, 2))
    if fmt == "e4m3":
        words = by_word.astype(ml_dtypes.float8_e4m3fn).view(np.uint8)
    else:
        c = by_word.astype(ml_dtypes.float4_e2m1fn).view(np.uint8) & 0xF
        words = c[..., 0::2] | (c[..., 1::2] << 4)
    return np.ascontiguousarray(words), np.ascontiguousarray(byte.astype(np.uint8).reshape(k // 512, 16, n))


def unpack_weight(words, scales, fmt):
    g, p, n, _ = words.shape
    if fmt == "e4m3":
        vals = np.ascontiguousarray(words).view(ml_dtypes.float8_e4m3fn).astype(np.float64)
    else:
        nib = np.empty((g, p, n, 4), np.uint8)
        nib[..., 0::2] = words & 0xF
        nib[..., 1::2] = words >> 4
        vals = E2M1[nib]
    vals = vals * np.repeat(np.exp2(scales.astype(np.float64) - 127.0), 8, axis=1)[..., None]
    return vals.transpose(0, 1, 3, 2).reshape(g * 512, n)
def pack4(w):
    words, scales = pack_weight(w, "e2m1")
    return words.reshape(words.shape[0], 128, -1), scales


def unpack4(words, scales):
    return unpack_weight(words.reshape(words.shape[0], 128, -1, 2), scales, "e2m1")


N, D, H, O, P = 1024, 1024, 1024, 1024, 2


def sigmoid(v):
    return 1.0 / (1.0 + np.exp(-v))


def jacobi_degree_one(u, alpha, beta):
    return (alpha + 1.0) + (alpha + beta + 2.0) * u


def jacobi_degree_two(u, alpha, beta):
    c0 = (alpha + 1.0) * (alpha + 2.0) / 2.0
    c1 = (alpha + 2.0) * (alpha + beta + 3.0)
    c2 = (alpha + beta + 3.0) * (alpha + beta + 4.0) / 2.0
    return c0 + c1 * u + c2 * (u * u)


def draw0():
    s = mx_kscale(D)
    t = np.stack([mx_kscale(H) for _ in range(P)])
    x = bf(np.random.standard_normal((N, D)) * s)
    w1_words, w1_scales = pack4(np.random.standard_normal((D, H)) * 1.5 / np.sqrt(D) / s[:, None])
    return {
        "x": x,
        "w1_words": w1_words,
        "w1_scales": w1_scales,
        "gamma": bf(np.random.uniform(0.6, 1.6, H)),
        "alpha": bf(np.random.uniform(0.0, 1.0, H)),
        "beta": bf(np.random.uniform(0.0, 1.0, H)),
        "g": bf((1.0 + 0.1 * np.random.standard_normal((P, H))) * t),
        "w2": bf(np.random.standard_normal((P, H, O)) / np.sqrt(H) / t[:, :, None]),
    }


def core(x, w1_words, w1_scales, gamma, alpha, beta, g, w2):
    z = mxq(f64(x), 1, "e4m3") @ unpack4(w1_words, w1_scales)

    u = np.power(sigmoid(z), f64(gamma)[None, :]) - 1.0

    a = f64(alpha)[None, :]
    b = f64(beta)[None, :]
    p1 = jacobi_degree_one(u, a, b)
    p2 = jacobi_degree_two(u, a, b)

    gain = f64(g)
    r1 = p1 * gain[0][None, :]
    r2 = p2 * gain[1][None, :]

    w = f64(w2)
    y1 = mxq(r1, 1, "e4m3") @ mxq(w[0], 0, "e4m3")
    y2 = mxq(r2, 1, "e4m3") @ mxq(w[1], 0, "e4m3")
    return y1 + y2


def e4m3fn_bytes(y):
    return np.clip(np.asarray(y, np.float64), -448.0, 448.0).astype(np.float32).astype(ml_dtypes.float8_e4m3fn).view(np.uint8)


def e4m3fn_values(b):
    return np.asarray(b, np.uint8).view(ml_dtypes.float8_e4m3fn).astype(np.float64)


def setup_inputs():
    d = draw0()
    x0 = np.asarray(d['x']).astype(np.float64)
    s = (np.max(np.abs(x0), axis=(0,), keepdims=True) / 448.0).astype(np.float32)
    out = {}
    for k, v in d.items():
        if k == 'x':
            out['x_bytes'] = e4m3fn_bytes(x0 / s.astype(np.float64))
            out['x_scale'] = s
        else:
            out[k] = v
    return out


def reference(x_bytes, x_scale, w1_words, w1_scales, gamma, alpha, beta, g, w2):
    return core(e4m3fn_values(x_bytes) * x_scale.astype(np.float64), w1_words, w1_scales, gamma, alpha, beta, g, w2)

@@ -1,0 +1,371 @@
+from contextlib import ExitStack
+
+import concourse.mybir as mybir
+from concourse.masks import make_identity
+
+N, D, H, O = 1024, 1024, 1024, 1024
+FLOPS = 2 * N * D * H + 2 * 2 * N * H * O
+
+F32 = mybir.dt.float32
+BF16 = mybir.dt.bfloat16
+I32 = mybir.dt.int32
+U32 = mybir.dt.uint32
+U8 = mybir.dt.uint8
+FP8 = mybir.dt.float8_e4m3fn
+FP8X4 = mybir.dt.float8_e4m3fn_x4
+FP4X4 = mybir.dt.float4_e2m1fn_x4
+ACT = mybir.ActivationFunctionType
+ALU = mybir.AluOpType
+
+P = 128
+BANK = 512
+TILES = N // P
+CHUNKS = (256, 256, 256, 256)
+LN_FLOOR = 2.0 ** -63
+
+
+def tile_fractionaljacobikantwodegree_w4_kernel(
+    tc, x_bytes, x_scale, w1_words, w1_scales, gamma, alpha, beta, g, w2, out
+):
+    nc = tc.nc
+
+    with ExitStack() as ctx:
+        keep = ctx.enter_context(tc.tile_pool(name="keep", bufs=1))
+        work = ctx.enter_context(tc.tile_pool(name="work", bufs=3))
+        psum = ctx.enter_context(tc.psum_pool(name="psum", bufs=1))
+        ctx.enter_context(tc.manual_schedule())
+
+        def bank(i):
+            return psum.tile([P, BANK], F32, name="bank%d" % i, tag="bank%d" % i)
+
+        def interleave(dst, src):
+            nc.vector.tensor_copy(
+                out=dst.rearrange("p (c i t) -> p c t i", i=4, t=4),
+                in_=src.rearrange("p t (c i) -> p c t i", i=4),
+            )
+
+        def quantize(codes, scales, src):
+            nc.vector.quantize_mx(out=codes.bitcast(FP8X4), scales=scales, in_=src)
+
+        warm = keep.tile([P, 1], F32)
+        nc.vector.memset(warm[:], 0.0)
+        w1s_raw = keep.tile([P, 2, H], U8)
+        nc.vector.memset(w1s_raw[:].bitcast(I32), 0)
+        warm_out = keep.tile([P, 1], F32)
+        nc.scalar.activation(out=warm_out[:], in_=warm[:], func=ACT.Sigmoid)
+        ident = keep.tile([P, P], F32)
+        make_identity(nc, ident[:])
+        par_raw = keep.tile([P, 2 * P], BF16)
+        nc.gpsimd.memset(par_raw[:], 0.0)
+
+        x_rows = x_bytes.rearrange("(p j) k -> p j k", j=TILES)
+        xb = [keep.tile([P, 2, D], U8, name="xb%d" % q) for q in range(4)]
+        xsc = keep.tile([P, 2, 4], F32)
+        w1_raw = keep.tile([P, 2, 2 * H], U8)
+        nc.sync.dma_start(out=xb[0][:], in_=x_rows[:, 0:2, :])
+        with nc.allow_non_contiguous_dma(reason="small vectors"):
+            nc.sync.dma_start(out=xsc[:], in_=x_scale.rearrange("o (g p t) -> p (o g) t", p=P, t=4))
+        nc.sync.dma_start(out=xb[1][:], in_=x_rows[:, 2:4, :])
+        nc.sync.dma_start(out=w1_raw[:].bitcast(I32), in_=w1_words.rearrange("g p b -> p g b").bitcast(I32))
+        nc.sync.dma_start(out=xb[2][:], in_=x_rows[:, 4:6, :])
+        nc.sync.dma_start(out=xb[3][:], in_=x_rows[:, 6:8, :])
+        for quad in range(4):
+            nc.sync.dma_start(
+                out=w1s_raw[32 * quad : 32 * quad + 4, :, :].bitcast(I32),
+                in_=w1_scales[:, 4 * quad : 4 * quad + 4, :].rearrange("g r n -> r g n").bitcast(I32),
+            )
+        w2_raw = {}
+        for gh in range(2):
+            for d in range(2):
+                w2_raw[d, gh] = keep.tile([P, 4, O], BF16, name="w2raw%d%d" % (d, gh))
+                rows = w2[d, 512 * gh : 512 * (gh + 1), :].rearrange("(a t e) n -> e a t n", t=4, e=4)
+                for e in range(4):
+                    nc.sync.dma_start(out=w2_raw[d, gh][e:P:4, :, :], in_=rows[e])
+        with nc.allow_non_contiguous_dma(reason="small vectors"):
+            for v, vec in enumerate((gamma, alpha, beta, g[0], g[1])):
+                nc.sync.dma_start(
+                    out=par_raw[4 * v : 4 * v + 4, :].rearrange("t (a e) -> t a e", e=4),
+                    in_=vec.rearrange("(a t e) -> t a e", t=4, e=4),
+                )
+
+        xw = [keep.tile([P, D], BF16, name="xw%d" % j) for j in range(TILES)]
+
+        def widen(j):
+            src = xb[j // 2][:, j % 2, :].bitcast(FP8)
+            if j == 0:
+                nc.vector.tensor_copy(out=xw[j][:], in_=src)
+            else:
+                nc.scalar.copy(out=xw[j][:], in_=src)
+
+        xt = {}
+
+        def turn(q):
+            for gk in range(2):
+                xt[q, gk] = bank((2 * q + gk) % 4)
+            for jj in range(2):
+                words = xw[2 * q + jj][:].bitcast(F32)
+                for gk in range(2):
+                    for u in range(2):
+                        col = 256 * u + P * jj
+                        nc.tensor.transpose(
+                            xt[q, gk][:, col : col + P], words[:, 256 * gk + u : 256 * (gk + 1) : 2], ident[:]
+                        )
+
+        xq = {}
+
+        def scale_x(q, gk):
+            xq[q, gk] = work.tile([P, 1024], BF16, name="xq", bufs=4, align_bytes=64)
+            nc.vector.tensor_tensor(
+                out=xq[q, gk][:].rearrange("p (n u e) -> p n u e", u=2, e=2),
+                in0=xt[q, gk][:].bitcast(BF16).rearrange("p (u n e) -> p n u e", u=2, e=2),
+                in1=xsc[:, gk, :].rearrange("p (u e) -> p u e", e=2).unsqueeze(1).to_broadcast([P, 256, 2, 2]),
+                op=ALU.mult,
+            )
+
+        x_codes = [keep.tile([P, N], U32, name="xcodes%d" % gk, align_bytes=64) for gk in range(2)]
+        x_scales = [keep.tile([P, N], U8, name="xscales%d" % gk, align_bytes=64) for gk in range(2)]
+
+        def quantize_x(q, gk):
+            cols = slice(256 * q, 256 * (q + 1))
+            quantize(x_codes[gk][:, cols], x_scales[gk][:, cols], xq[q, gk][:])
+
+        w1c = keep.tile([P, 2, 2 * H], U8, align_bytes=64)
+        w1s = keep.tile([P, 2, H], U8, align_bytes=64)
+
+        def order_w1_codes():
+            nc.vector.tensor_copy(
+                out=w1c[:].bitcast(I32).rearrange("p g (h t a e) -> p (g h) t a e", h=2, t=4, e=2),
+                in_=w1_raw[:].bitcast(I32).rearrange("p g (h a t e) -> p (g h) t a e", h=2, t=4, e=2),
+            )
+
+        def order_w1_scales():
+            nc.vector.tensor_copy(
+                out=w1s[:].bitcast(I32).rearrange("p g (h t a) -> p (g h) t a", h=2, t=4),
+                in_=w1s_raw[:].bitcast(I32).rearrange("p g (h a t) -> p (g h) t a", h=2, t=4),
+            )
+
+        z = {}
+
+        def project(half, ht, gk):
+            if gk == 0:
+                z[half, ht] = bank(4 + ht % 4)
+            cols = slice(BANK * half, BANK * (half + 1))
+            nc.tensor.matmul_mx(
+                out=z[half, ht][:],
+                lhsT=w1c[:, gk, 2 * P * ht : 2 * P * (ht + 1)].bitcast(FP4X4),
+                lhsT_scale=w1s[:, gk, P * ht : P * (ht + 1)],
+                rhs=x_codes[gk][:, cols].bitcast(FP8X4),
+                rhs_scale=x_scales[gk][:, cols],
+                start=(gk == 0),
+                stop=(gk == 1),
+            )
+
+        s = keep.tile([P, 8, N], F32)
+
+        def sigmoid(half, ht):
+            nc.scalar.activation(out=s[:, ht, BANK * half : BANK * (half + 1)], in_=z[half, ht][:], func=ACT.Sigmoid)
+
+        for j in range(TILES):
+            widen(j)
+        turn(0)
+        turn(1)
+        scale_x(0, 0)
+        order_w1_codes()
+        scale_x(0, 1)
+        quantize_x(0, 0)
+        turn(2)
+        scale_x(1, 0)
+        quantize_x(0, 1)
+        order_w1_scales()
+        scale_x(1, 1)
+        quantize_x(1, 0)
+        quantize_x(1, 1)
+        for gk in range(2):
+            for ht in range(4):
+                project(0, ht, gk)
+        turn(3)
+        scale_x(2, 0)
+        scale_x(2, 1)
+        quantize_x(2, 0)
+        scale_x(3, 0)
+        quantize_x(2, 1)
+        scale_x(3, 1)
+        quantize_x(3, 0)
+        quantize_x(3, 1)
+        for ht in range(4):
+            sigmoid(0, ht)
+        for half, first in ((0, 4), (1, 0)):
+            for ht in range(first, 8):
+                for gk in range(2):
+                    project(half, ht, gk)
+                sigmoid(half, ht)
+
+        for pair in range(4):
+            both = s[:, 2 * pair : 2 * pair + 2, :]
+            nc.scalar.activation(out=both, in_=both, func=ACT.Ln, bias=LN_FLOOR)
+
+        par_f32 = keep.tile([P, 2 * P], F32)
+        par = keep.tile([P, 2, 32], F32)
+        cst = {name: keep.tile([P, 2, 4], F32, name=name) for name in
+               ("s4", "rec", "nb2", "h", "a1", "b1", "t1", "a2", "t2", "k2")}
+        ga, al, be, g0, g1 = [par[:, :, 4 * v : 4 * v + 4] for v in range(5)]
+
+        def stt(name, in0, scalar, in1, op0, op1):
+            nc.vector.scalar_tensor_tensor(out=cst[name][:], in0=in0, scalar=scalar, in1=in1, op0=op0, op1=op1)
+
+        def par_widen():
+            nc.vector.tensor_copy(out=par_f32[:], in_=par_raw[:])
+
+        def par_turn():
+            par_t = bank(0)
+            for gh in range(2):
+                nc.tensor.transpose(par_t[:, P * gh : P * (gh + 1)], par_f32[:, P * gh : P * (gh + 1)], ident[:])
+            nc.vector.tensor_copy(out=par[:], in_=par_t[:, 0 : 2 * P].rearrange("p (g c) -> p g c", g=2)[:, :, 0:32])
+
+        def par_first():
+            stt("s4", al, 4.0, be, ALU.add, ALU.add)
+            nc.vector.tensor_scalar(out=cst["nb2"][:], in0=be, scalar1=2.0, scalar2=-1.0, op0=ALU.add, op1=ALU.mult)
+            stt("b1", be, 1.0, g0, ALU.add, ALU.mult)
+
+        def par_second():
+            nc.vector.reciprocal(out=cst["rec"][:], in_=cst["s4"][:])
+            stt("a1", cst["s4"][:], -2.0, g0, ALU.add, ALU.mult)
+            stt("t1", cst["s4"][:], -1.0, cst["s4"][:], ALU.add, ALU.mult)
+
+        def par_third():
+            nc.vector.tensor_tensor(out=cst["h"][:], in0=cst["nb2"][:], in1=cst["rec"][:], op=ALU.mult)
+            stt("a2", cst["t1"][:], 0.5, g1, ALU.mult, ALU.mult)
+
+        def par_fourth():
+            stt("t2", al, 2.0, cst["h"][:], ALU.add, ALU.mult)
+
+        def par_fifth():
+            stt("k2", cst["t2"][:], 0.5, g1, ALU.mult, ALU.mult)
+
+        par_steps = [par_widen, par_turn, par_first, par_second, par_third, par_fourth, par_fifth]
+
+        w2_codes = {}
+        w2_scales = {}
+        for gh in range(2):
+            for d in range(2):
+                w2_codes[d, gh] = keep.tile([P, O], U32, name="w2codes%d%d" % (d, gh), align_bytes=64)
+                w2_scales[d, gh] = keep.tile([P, O], U8, name="w2scales%d%d" % (d, gh), align_bytes=64)
+        pieces = [(d, gh, half) for gh in range(2) for d in range(2) for half in range(2)]
+        w2q = {}
+        for i in range(len(pieces) + 1):
+            if i < len(pieces):
+                d, gh, half = pieces[i]
+                w2q[i] = work.tile([P, 4 * BANK], BF16, name="w2q", align_bytes=64)
+                interleave(w2q[i][:], w2_raw[d, gh][:, :, BANK * half : BANK * (half + 1)])
+            if i >= 2:
+                par_steps[i - 2]()
+            if i >= 1:
+                d, gh, half = pieces[i - 1]
+                cols = slice(BANK * half, BANK * (half + 1))
+                quantize(w2_codes[d, gh][:, cols], w2_scales[d, gh][:, cols], w2q[i - 1][:])
+
+        out_rows = out.rearrange("(p j) o -> p j o", j=TILES)
+        starts = [sum(CHUNKS[:c]) for c in range(len(CHUNKS))]
+        steps = [(c, gh) for c in range(len(CHUNKS)) for gh in range(2)]
+        vt = {}
+        qt = {}
+        acc = {}
+
+        def power(c, gh, t):
+            vt[c, gh, t] = work.tile([P, CHUNKS[c]], F32, name="v", bufs=8)
+            nc.scalar.activation(
+                out=vt[c, gh, t][:], in_=s[:, 4 * gh + t, starts[c] : starts[c] + CHUNKS[c]],
+                func=ACT.Exp, scale=ga[:, gh, t : t + 1],
+            )
+
+        def square(c, gh, t):
+            qt[c, gh, t] = work.tile([P, CHUNKS[c]], F32, name="q", bufs=8)
+            nc.scalar.activation(
+                out=qt[c, gh, t][:], in_=vt[c, gh, t][:], func=ACT.Square, bias=cst["h"][:, gh, t : t + 1]
+            )
+
+        def degree_one(plane, c, gh, t):
+            nc.vector.tensor_scalar(
+                out=plane[:, t, :], in0=vt[c, gh, t][:], scalar1=cst["a1"][:, gh, t : t + 1],
+                scalar2=cst["b1"][:, gh, t : t + 1], op0=ALU.mult, op1=ALU.subtract,
+            )
+
+        def degree_two(plane, c, gh, t):
+            nc.vector.tensor_scalar(
+                out=plane[:, t, :], in0=qt[c, gh, t][:], scalar1=cst["a2"][:, gh, t : t + 1],
+                scalar2=cst["k2"][:, gh, t : t + 1], op0=ALU.mult, op1=ALU.add,
+            )
+
+        def multiply(c, gh, d, rq):
+            codes = work.tile([P, CHUNKS[c]], U32, name="rcodes", bufs=4, align_bytes=64)
+            scales = work.tile([P, CHUNKS[c]], U8, name="rscales", bufs=4, align_bytes=64)
+            quantize(codes[:], scales[:], rq[:])
+            for jj in range(CHUNKS[c] // P):
+                j = starts[c] // P + jj
+                for half in range(2):
+                    if gh == 0 and d == 0:
+                        acc[j, half] = bank((2 * j + half) % 8)
+                    cols = slice(BANK * half, BANK * (half + 1))
+                    nc.tensor.matmul_mx(
+                        out=acc[j, half][:],
+                        lhsT=codes[:, P * jj : P * (jj + 1)].bitcast(FP8X4),
+                        lhsT_scale=scales[:, P * jj : P * (jj + 1)],
+                        rhs=w2_codes[d, gh][:, cols].bitcast(FP8X4),
+                        rhs_scale=w2_scales[d, gh][:, cols],
+                        start=(gh == 0 and d == 0),
+                        stop=(gh == 1 and d == 1),
+                    )
+
+        def store(j, half, on_vector):
+            y = work.tile([P, BANK], F32, name="y", bufs=4)
+            if on_vector:
+                nc.vector.tensor_copy(out=y[:], in_=acc[j, half][:])
+            else:
+                nc.scalar.copy(out=y[:], in_=acc[j, half][:])
+            nc.sync.dma_start(out=out_rows[:, j, BANK * half : BANK * (half + 1)], in_=y[:])
+
+        def banks_of(c):
+            return [(starts[c] // P + jj, half) for jj in range(CHUNKS[c] // P) for half in range(2)]
+
+        def scalar_step(i):
+            c, gh = steps[i]
+            power(c, gh, 0)
+            if i > 0:
+                square(steps[i - 1][0], steps[i - 1][1], 3)
+            for t in range(1, 4):
+                power(c, gh, t)
+                square(c, gh, t - 1)
+            if i == len(steps) - 1:
+                square(c, gh, 3)
+
+        held = None
+        scalar_step(0)
+        for i, (c, gh) in enumerate(steps):
+            if i + 1 < len(steps):
+                scalar_step(i + 1)
+            r1 = work.tile([P, 4, CHUNKS[c]], BF16, name="r1")
+            r2 = work.tile([P, 4, CHUNKS[c]], BF16, name="r2")
+            degree_one(r1, c, gh, 0)
+            if held is not None:
+                multiply(*held)
+            if c > 0 and gh == 0:
+                for j, half in banks_of(c - 1)[1:]:
+                    store(j, half, False)
+            degree_one(r1, c, gh, 1)
+            degree_two(r2, c, gh, 0)
+            degree_one(r1, c, gh, 2)
+            degree_two(r2, c, gh, 1)
+            degree_one(r1, c, gh, 3)
+            degree_two(r2, c, gh, 2)
+            rq1 = work.tile([P, 4 * CHUNKS[c]], BF16, name="rq", bufs=3, align_bytes=64)
+            interleave(rq1[:], r1[:])
+            degree_two(r2, c, gh, 3)
+            if c > 0 and gh == 0:
+                store(banks_of(c - 1)[0][0], banks_of(c - 1)[0][1], True)
+            multiply(c, gh, 0, rq1)
+            rq2 = work.tile([P, 4 * CHUNKS[c]], BF16, name="rq", bufs=3, align_bytes=64)
+            interleave(rq2[:], r2[:])
+            held = (c, gh, 1, rq2)
+        multiply(*held)
+        for n, (j, half) in enumerate(banks_of(len(CHUNKS) - 1)):
+            store(j, half, n % 2 == 1)

@@ -20,8 +20,12 @@ ALU = mybir.AluOpType
 P = 128
 BANK = 512
 TILES = N // P
-CHUNKS = (256, 256, 256, 256)
+CHUNKS = (256, 256, 256, 128, 128)
 LN_FLOOR = 2.0 ** -63
+VECTOR_WIDENS = (0, 2)
+WARM_HEAD = 5
+WARM_EACH = 2
+DRAIN = 2
 
 
 def tile_fractionaljacobikantwodegree_w4_kernel(
@@ -53,6 +57,8 @@ def tile_fractionaljacobikantwodegree_w4_kernel(
         nc.vector.memset(w1s_raw[:].bitcast(I32), 0)
         warm_out = keep.tile([P, 1], F32)
         nc.scalar.activation(out=warm_out[:], in_=warm[:], func=ACT.Sigmoid)
+        idle = keep.tile([P, BANK], BF16)
+        nc.vector.memset(idle[:], 0.0)
         ident = keep.tile([P, P], F32)
         make_identity(nc, ident[:])
         par_raw = keep.tile([P, 2 * P], BF16)
@@ -92,7 +98,7 @@ def tile_fractionaljacobikantwodegree_w4_kernel(
 
         def widen(j):
             src = xb[j // 2][:, j % 2, :].bitcast(FP8)
-            if j == 0:
+            if j in VECTOR_WIDENS:
                 nc.vector.tensor_copy(out=xw[j][:], in_=src)
             else:
                 nc.scalar.copy(out=xw[j][:], in_=src)
@@ -101,10 +107,10 @@ def tile_fractionaljacobikantwodegree_w4_kernel(
 
         def turn(q):
             for gk in range(2):
-                xt[q, gk] = bank((2 * q + gk) % 4)
-            for jj in range(2):
-                words = xw[2 * q + jj][:].bitcast(F32)
-                for gk in range(2):
+                xt[q, gk] = bank((2 * q + gk) % 5)
+            for gk in range(2):
+                for jj in range(2):
+                    words = xw[2 * q + jj][:].bitcast(F32)
                     for u in range(2):
                         col = 256 * u + P * jj
                         nc.tensor.transpose(
@@ -148,7 +154,7 @@ def tile_fractionaljacobikantwodegree_w4_kernel(
 
         def project(half, ht, gk):
             if gk == 0:
-                z[half, ht] = bank(4 + ht % 4)
+                z[half, ht] = bank(5 + (8 * half + ht) % 3)
             cols = slice(BANK * half, BANK * (half + 1))
             nc.tensor.matmul_mx(
                 out=z[half, ht][:],
@@ -165,25 +171,31 @@ def tile_fractionaljacobikantwodegree_w4_kernel(
         def sigmoid(half, ht):
             nc.scalar.activation(out=s[:, ht, BANK * half : BANK * (half + 1)], in_=z[half, ht][:], func=ACT.Sigmoid)
 
+        def warm_tensor(count):
+            scratch = bank(7)
+            for n in range(count):
+                nc.tensor.matmul(scratch[:], lhsT=idle[:, 0:P], rhs=idle[:], start=True, stop=True)
+
+        warm_tensor(WARM_HEAD)
         for j in range(TILES):
             widen(j)
         turn(0)
+        warm_tensor(WARM_EACH)
         turn(1)
+        warm_tensor(WARM_EACH)
         scale_x(0, 0)
         order_w1_codes()
         scale_x(0, 1)
         quantize_x(0, 0)
         turn(2)
+        warm_tensor(WARM_EACH)
         scale_x(1, 0)
         quantize_x(0, 1)
         order_w1_scales()
         scale_x(1, 1)
+        turn(3)
         quantize_x(1, 0)
         quantize_x(1, 1)
-        for gk in range(2):
-            for ht in range(4):
-                project(0, ht, gk)
-        turn(3)
         scale_x(2, 0)
         scale_x(2, 1)
         quantize_x(2, 0)
@@ -192,10 +204,8 @@ def tile_fractionaljacobikantwodegree_w4_kernel(
         scale_x(3, 1)
         quantize_x(3, 0)
         quantize_x(3, 1)
-        for ht in range(4):
-            sigmoid(0, ht)
-        for half, first in ((0, 4), (1, 0)):
-            for ht in range(first, 8):
+        for half in range(2):
+            for ht in range(8):
                 for gk in range(2):
                     project(half, ht, gk)
                 sigmoid(half, ht)
@@ -317,7 +327,7 @@ def tile_fractionaljacobikantwodegree_w4_kernel(
                     )
 
         def store(j, half, on_vector):
-            y = work.tile([P, BANK], F32, name="y", bufs=4)
+            y = work.tile([P, BANK], F32, name="y", bufs=8)
             if on_vector:
                 nc.vector.tensor_copy(out=y[:], in_=acc[j, half][:])
             else:
@@ -338,34 +348,52 @@ def tile_fractionaljacobikantwodegree_w4_kernel(
             if i == len(steps) - 1:
                 square(c, gh, 3)
 
-        held = None
+        def ready(r):
+            rq = work.tile([P, 4 * r.shape[2]], BF16, name="rq", bufs=3, align_bytes=64)
+            interleave(rq[:], r[:])
+            return rq
+
+        last = len(steps) - 1
+        planes = {}
+        full = []
+
+        def drain(count, on_vector):
+            for j, half in full[:count]:
+                store(j, half, on_vector)
+                full.remove((j, half))
+
         scalar_step(0)
         for i, (c, gh) in enumerate(steps):
-            if i + 1 < len(steps):
+            if i < last:
                 scalar_step(i + 1)
+            drain(DRAIN, False)
             r1 = work.tile([P, 4, CHUNKS[c]], BF16, name="r1")
             r2 = work.tile([P, 4, CHUNKS[c]], BF16, name="r2")
+            planes[i] = (r1, r2)
             degree_one(r1, c, gh, 0)
-            if held is not None:
-                multiply(*held)
-            if c > 0 and gh == 0:
-                for j, half in banks_of(c - 1)[1:]:
-                    store(j, half, False)
+            if i > 0:
+                pc, pgh = steps[i - 1]
+                rq1 = ready(planes[i - 1][0])
             degree_one(r1, c, gh, 1)
             degree_two(r2, c, gh, 0)
+            if i > 0:
+                rq2 = ready(planes[i - 1][1])
             degree_one(r1, c, gh, 2)
+            if i > 0:
+                multiply(pc, pgh, 0, rq1)
             degree_two(r2, c, gh, 1)
             degree_one(r1, c, gh, 3)
+            if i > 0:
+                multiply(pc, pgh, 1, rq2)
             degree_two(r2, c, gh, 2)
-            rq1 = work.tile([P, 4 * CHUNKS[c]], BF16, name="rq", bufs=3, align_bytes=64)
-            interleave(rq1[:], r1[:])
+            if i == last:
+                rq1 = ready(r1)
             degree_two(r2, c, gh, 3)
-            if c > 0 and gh == 0:
-                store(banks_of(c - 1)[0][0], banks_of(c - 1)[0][1], True)
-            multiply(c, gh, 0, rq1)
-            rq2 = work.tile([P, 4 * CHUNKS[c]], BF16, name="rq", bufs=3, align_bytes=64)
-            interleave(rq2[:], r2[:])
-            held = (c, gh, 1, rq2)
-        multiply(*held)
-        for n, (j, half) in enumerate(banks_of(len(CHUNKS) - 1)):
+            if i > 0 and pgh == 1:
+                full.extend(banks_of(pc))
+        multiply(c, gh, 0, rq1)
+        rq2 = ready(r2)
+        drain(len(full), False)
+        multiply(c, gh, 1, rq2)
+        for n, (j, half) in enumerate(banks_of(c)):
             store(j, half, n % 2 == 1)

@@ -20,7 +20,7 @@ ALU = mybir.AluOpType
 P = 128
 BANK = 512
 TILES = N // P
-CHUNKS = (256, 256, 256, 128, 128)
+CHUNKS = (128, 256, 256, 256, 128)
 LN_FLOOR = 2.0 ** -63
 VECTOR_WIDENS = (0, 2)
 WARM_HEAD = 5
@@ -55,13 +55,11 @@ def tile_fractionaljacobikantwodegree_w4_kernel(
         nc.vector.memset(warm[:], 0.0)
         w1s_raw = keep.tile([P, 2, H], U8)
         nc.vector.memset(w1s_raw[:].bitcast(I32), 0)
-        warm_out = keep.tile([P, 1], F32)
-        nc.scalar.activation(out=warm_out[:], in_=warm[:], func=ACT.Sigmoid)
         idle = keep.tile([P, BANK], BF16)
         nc.vector.memset(idle[:], 0.0)
         ident = keep.tile([P, P], F32)
         make_identity(nc, ident[:])
-        par_raw = keep.tile([P, 2 * P], BF16)
+        par_raw = keep.tile([P, BANK], BF16)
         nc.gpsimd.memset(par_raw[:], 0.0)
 
         x_rows = x_bytes.rearrange("(p j) k -> p j k", j=TILES)
@@ -70,7 +68,9 @@ def tile_fractionaljacobikantwodegree_w4_kernel(
         w1_raw = keep.tile([P, 2, 2 * H], U8)
         nc.sync.dma_start(out=xb[0][:], in_=x_rows[:, 0:2, :])
         with nc.allow_non_contiguous_dma(reason="small vectors"):
-            nc.sync.dma_start(out=xsc[:], in_=x_scale.rearrange("o (g p t) -> p (o g) t", p=P, t=4))
+            nc.scalar.dma_start(out=xsc[:], in_=x_scale.rearrange("o (g p t) -> p (o g) t", p=P, t=4))
+        warm_out = keep.tile([P, 1], F32)
+        nc.scalar.activation(out=warm_out[:], in_=warm[:], func=ACT.Sigmoid)
         nc.sync.dma_start(out=xb[1][:], in_=x_rows[:, 2:4, :])
         nc.sync.dma_start(out=w1_raw[:].bitcast(I32), in_=w1_words.rearrange("g p b -> p g b").bitcast(I32))
         nc.sync.dma_start(out=xb[2][:], in_=x_rows[:, 4:6, :])
@@ -87,12 +87,9 @@ def tile_fractionaljacobikantwodegree_w4_kernel(
                 rows = w2[d, 512 * gh : 512 * (gh + 1), :].rearrange("(a t e) n -> e a t n", t=4, e=4)
                 for e in range(4):
                     nc.sync.dma_start(out=w2_raw[d, gh][e:P:4, :, :], in_=rows[e])
-        with nc.allow_non_contiguous_dma(reason="small vectors"):
-            for v, vec in enumerate((gamma, alpha, beta, g[0], g[1])):
-                nc.sync.dma_start(
-                    out=par_raw[4 * v : 4 * v + 4, :].rearrange("t (a e) -> t a e", e=4),
-                    in_=vec.rearrange("(a t e) -> t a e", t=4, e=4),
-                )
+        for v, vec in enumerate((gamma, alpha, beta)):
+            nc.sync.dma_start(out=par_raw[2 * v : 2 * v + 2, :], in_=vec.rearrange("(h c) -> h c", h=2))
+        nc.sync.dma_start(out=par_raw[6:10, :], in_=g.rearrange("d (h c) -> (d h) c", h=2))
 
         xw = [keep.tile([P, D], BF16, name="xw%d" % j) for j in range(TILES)]
 
@@ -127,6 +124,19 @@ def tile_fractionaljacobikantwodegree_w4_kernel(
                 in1=xsc[:, gk, :].rearrange("p (u e) -> p u e", e=2).unsqueeze(1).to_broadcast([P, 256, 2, 2]),
                 op=ALU.mult,
             )
+
+        def scale_x_planes(q, gk):
+            planes = keep.tile([P, 4, 256], BF16)
+            turned = xt[q, gk][:].bitcast(BF16).rearrange("p (u n e) -> p u e n", u=2, e=2)
+            for t in range(4):
+                nc.scalar.activation(
+                    out=planes[:, t, :], in_=turned[:, t // 2, t % 2, :], func=ACT.Copy, scale=xsc[:, gk, t : t + 1]
+                )
+            return planes
+
+        def interleave_x(q, gk, planes):
+            xq[q, gk] = work.tile([P, 1024], BF16, name="xq", bufs=4, align_bytes=64)
+            interleave(xq[q, gk][:], planes[:])
 
         x_codes = [keep.tile([P, N], U32, name="xcodes%d" % gk, align_bytes=64) for gk in range(2)]
         x_scales = [keep.tile([P, N], U8, name="xscales%d" % gk, align_bytes=64) for gk in range(2)]
@@ -196,11 +206,12 @@ def tile_fractionaljacobikantwodegree_w4_kernel(
         turn(3)
         quantize_x(1, 0)
         quantize_x(1, 1)
-        scale_x(2, 0)
+        planes = scale_x_planes(2, 0)
         scale_x(2, 1)
-        quantize_x(2, 0)
-        scale_x(3, 0)
+        interleave_x(2, 0, planes)
         quantize_x(2, 1)
+        scale_x(3, 0)
+        quantize_x(2, 0)
         scale_x(3, 1)
         quantize_x(3, 0)
         quantize_x(3, 1)
@@ -214,23 +225,26 @@ def tile_fractionaljacobikantwodegree_w4_kernel(
             both = s[:, 2 * pair : 2 * pair + 2, :]
             nc.scalar.activation(out=both, in_=both, func=ACT.Ln, bias=LN_FLOOR)
 
-        par_f32 = keep.tile([P, 2 * P], F32)
-        par = keep.tile([P, 2, 32], F32)
-        cst = {name: keep.tile([P, 2, 4], F32, name=name) for name in
+        par_f32 = keep.tile([P, BANK], F32)
+        par = keep.tile([P, 4, 16], F32)
+        cst = {name: keep.tile([P, 4, 2], F32, name=name) for name in
                ("s4", "rec", "nb2", "h", "a1", "b1", "t1", "a2", "t2", "k2")}
-        ga, al, be, g0, g1 = [par[:, :, 4 * v : 4 * v + 4] for v in range(5)]
+        ga, al, be, g0, g1 = [par[:, :, 2 * v : 2 * v + 2] for v in range(5)]
 
         def stt(name, in0, scalar, in1, op0, op1):
             nc.vector.scalar_tensor_tensor(out=cst[name][:], in0=in0, scalar=scalar, in1=in1, op0=op0, op1=op1)
 
         def par_widen():
-            nc.vector.tensor_copy(out=par_f32[:], in_=par_raw[:])
+            nc.vector.tensor_copy(
+                out=par_f32[:].rearrange("p (t a e) -> p t a e", t=4, e=4),
+                in_=par_raw[:].rearrange("p (a t e) -> p t a e", t=4, e=4),
+            )
 
         def par_turn():
             par_t = bank(0)
-            for gh in range(2):
-                nc.tensor.transpose(par_t[:, P * gh : P * (gh + 1)], par_f32[:, P * gh : P * (gh + 1)], ident[:])
-            nc.vector.tensor_copy(out=par[:], in_=par_t[:, 0 : 2 * P].rearrange("p (g c) -> p g c", g=2)[:, :, 0:32])
+            for t in range(4):
+                nc.tensor.transpose(par_t[:, P * t : P * (t + 1)], par_f32[:, P * t : P * (t + 1)], ident[:])
+            nc.vector.tensor_copy(out=par[:], in_=par_t[:].rearrange("p (t c) -> p t c", t=4)[:, :, 0:16])
 
         def par_first():
             stt("s4", al, 4.0, be, ALU.add, ALU.add)
@@ -262,17 +276,24 @@ def tile_fractionaljacobikantwodegree_w4_kernel(
                 w2_scales[d, gh] = keep.tile([P, O], U8, name="w2scales%d%d" % (d, gh), align_bytes=64)
         pieces = [(d, gh, half) for gh in range(2) for d in range(2) for half in range(2)]
         w2q = {}
-        for i in range(len(pieces) + 1):
-            if i < len(pieces):
-                d, gh, half = pieces[i]
-                w2q[i] = work.tile([P, 4 * BANK], BF16, name="w2q", align_bytes=64)
-                interleave(w2q[i][:], w2_raw[d, gh][:, :, BANK * half : BANK * (half + 1)])
-            if i >= 2:
-                par_steps[i - 2]()
-            if i >= 1:
-                d, gh, half = pieces[i - 1]
-                cols = slice(BANK * half, BANK * (half + 1))
-                quantize(w2_codes[d, gh][:, cols], w2_scales[d, gh][:, cols], w2q[i - 1][:])
+
+        def interleave_w2(i):
+            d, gh, half = pieces[i]
+            w2q[i] = work.tile([P, 4 * BANK], BF16, name="w2q", align_bytes=64)
+            interleave(w2q[i][:], w2_raw[d, gh][:, :, BANK * half : BANK * (half + 1)])
+
+        def quantize_w2(i):
+            d, gh, half = pieces[i]
+            cols = slice(BANK * half, BANK * (half + 1))
+            quantize(w2_codes[d, gh][:, cols], w2_scales[d, gh][:, cols], w2q[i][:])
+
+        interleave_w2(0)
+        for i in range(len(pieces)):
+            if i + 1 < len(pieces):
+                interleave_w2(i + 1)
+            if i > 0:
+                par_steps[i - 1]()
+            quantize_w2(i)
 
         out_rows = out.rearrange("(p j) o -> p j o", j=TILES)
         starts = [sum(CHUNKS[:c]) for c in range(len(CHUNKS))]
@@ -285,46 +306,52 @@ def tile_fractionaljacobikantwodegree_w4_kernel(
             vt[c, gh, t] = work.tile([P, CHUNKS[c]], F32, name="v", bufs=8)
             nc.scalar.activation(
                 out=vt[c, gh, t][:], in_=s[:, 4 * gh + t, starts[c] : starts[c] + CHUNKS[c]],
-                func=ACT.Exp, scale=ga[:, gh, t : t + 1],
+                func=ACT.Exp, scale=ga[:, t, gh : gh + 1],
             )
 
         def square(c, gh, t):
             qt[c, gh, t] = work.tile([P, CHUNKS[c]], F32, name="q", bufs=8)
             nc.scalar.activation(
-                out=qt[c, gh, t][:], in_=vt[c, gh, t][:], func=ACT.Square, bias=cst["h"][:, gh, t : t + 1]
+                out=qt[c, gh, t][:], in_=vt[c, gh, t][:], func=ACT.Square, bias=cst["h"][:, t, gh : gh + 1]
             )
 
-        def degree_one(plane, c, gh, t):
+        def slot(pairs, d, t):
+            return pairs[:, d, t, :]
+
+        def degree_one(pairs, c, gh, t):
             nc.vector.tensor_scalar(
-                out=plane[:, t, :], in0=vt[c, gh, t][:], scalar1=cst["a1"][:, gh, t : t + 1],
-                scalar2=cst["b1"][:, gh, t : t + 1], op0=ALU.mult, op1=ALU.subtract,
+                out=slot(pairs, 0, t), in0=vt[c, gh, t][:], scalar1=cst["a1"][:, t, gh : gh + 1],
+                scalar2=cst["b1"][:, t, gh : gh + 1], op0=ALU.mult, op1=ALU.subtract,
             )
 
-        def degree_two(plane, c, gh, t):
+        def degree_two(pairs, c, gh, t):
             nc.vector.tensor_scalar(
-                out=plane[:, t, :], in0=qt[c, gh, t][:], scalar1=cst["a2"][:, gh, t : t + 1],
-                scalar2=cst["k2"][:, gh, t : t + 1], op0=ALU.mult, op1=ALU.add,
+                out=slot(pairs, 1, t), in0=qt[c, gh, t][:], scalar1=cst["a2"][:, t, gh : gh + 1],
+                scalar2=cst["k2"][:, t, gh : gh + 1], op0=ALU.mult, op1=ALU.add,
             )
 
-        def multiply(c, gh, d, rq):
-            codes = work.tile([P, CHUNKS[c]], U32, name="rcodes", bufs=4, align_bytes=64)
-            scales = work.tile([P, CHUNKS[c]], U8, name="rscales", bufs=4, align_bytes=64)
+        def multiply(c, gh, degrees, rq):
+            width = len(degrees) * CHUNKS[c]
+            codes = work.tile([P, width], U32, name="rcodes", align_bytes=64)
+            scales = work.tile([P, width], U8, name="rscales", align_bytes=64)
             quantize(codes[:], scales[:], rq[:])
             for jj in range(CHUNKS[c] // P):
                 j = starts[c] // P + jj
                 for half in range(2):
-                    if gh == 0 and d == 0:
-                        acc[j, half] = bank((2 * j + half) % 8)
                     cols = slice(BANK * half, BANK * (half + 1))
-                    nc.tensor.matmul_mx(
-                        out=acc[j, half][:],
-                        lhsT=codes[:, P * jj : P * (jj + 1)].bitcast(FP8X4),
-                        lhsT_scale=scales[:, P * jj : P * (jj + 1)],
-                        rhs=w2_codes[d, gh][:, cols].bitcast(FP8X4),
-                        rhs_scale=w2_scales[d, gh][:, cols],
-                        start=(gh == 0 and d == 0),
-                        stop=(gh == 1 and d == 1),
-                    )
+                    for n, d in enumerate(degrees):
+                        if gh == 0 and d == 0:
+                            acc[j, half] = bank((2 * j + half) % 8)
+                        toks = slice(CHUNKS[c] * n + P * jj, CHUNKS[c] * n + P * (jj + 1))
+                        nc.tensor.matmul_mx(
+                            out=acc[j, half][:],
+                            lhsT=codes[:, toks].bitcast(FP8X4),
+                            lhsT_scale=scales[:, toks],
+                            rhs=w2_codes[d, gh][:, cols].bitcast(FP8X4),
+                            rhs_scale=w2_scales[d, gh][:, cols],
+                            start=(gh == 0 and d == 0),
+                            stop=(gh == 1 and d == 1),
+                        )
 
         def store(j, half, on_vector):
             y = work.tile([P, BANK], F32, name="y", bufs=8)
@@ -348,13 +375,16 @@ def tile_fractionaljacobikantwodegree_w4_kernel(
             if i == len(steps) - 1:
                 square(c, gh, 3)
 
-        def ready(r):
-            rq = work.tile([P, 4 * r.shape[2]], BF16, name="rq", bufs=3, align_bytes=64)
-            interleave(rq[:], r[:])
+        def ready(pairs, degrees):
+            some = pairs[:, degrees[0] : degrees[-1] + 1, :, :]
+            rq = work.tile([P, 4 * len(degrees) * some.shape[3]], BF16, name="rq", align_bytes=64)
+            nc.vector.tensor_copy(
+                out=rq[:].rearrange("p (d c i t) -> p d c t i", d=len(degrees), i=4, t=4),
+                in_=some.rearrange("p d t (c i) -> p d c t i", i=4),
+            )
             return rq
 
         last = len(steps) - 1
-        planes = {}
         full = []
 
         def drain(count, on_vector):
@@ -363,37 +393,32 @@ def tile_fractionaljacobikantwodegree_w4_kernel(
                 full.remove((j, half))
 
         scalar_step(0)
+        before = None
         for i, (c, gh) in enumerate(steps):
             if i < last:
                 scalar_step(i + 1)
             drain(DRAIN, False)
-            r1 = work.tile([P, 4, CHUNKS[c]], BF16, name="r1")
-            r2 = work.tile([P, 4, CHUNKS[c]], BF16, name="r2")
-            planes[i] = (r1, r2)
-            degree_one(r1, c, gh, 0)
+            pairs = work.tile([P, 2, 4, CHUNKS[c]], BF16, name="pairs")
+            degree_one(pairs, c, gh, 0)
+            degree_one(pairs, c, gh, 1)
             if i > 0:
-                pc, pgh = steps[i - 1]
-                rq1 = ready(planes[i - 1][0])
-            degree_one(r1, c, gh, 1)
-            degree_two(r2, c, gh, 0)
+                rq = ready(before, (0, 1))
+            degree_two(pairs, c, gh, 0)
+            degree_one(pairs, c, gh, 2)
+            degree_two(pairs, c, gh, 1)
             if i > 0:
-                rq2 = ready(planes[i - 1][1])
-            degree_one(r1, c, gh, 2)
-            if i > 0:
-                multiply(pc, pgh, 0, rq1)
-            degree_two(r2, c, gh, 1)
-            degree_one(r1, c, gh, 3)
-            if i > 0:
-                multiply(pc, pgh, 1, rq2)
-            degree_two(r2, c, gh, 2)
+                multiply(steps[i - 1][0], steps[i - 1][1], (0, 1), rq)
+            degree_one(pairs, c, gh, 3)
+            degree_two(pairs, c, gh, 2)
             if i == last:
-                rq1 = ready(r1)
-            degree_two(r2, c, gh, 3)
-            if i > 0 and pgh == 1:
-                full.extend(banks_of(pc))
-        multiply(c, gh, 0, rq1)
-        rq2 = ready(r2)
+                rq = ready(pairs, (0,))
+            degree_two(pairs, c, gh, 3)
+            if i > 0 and gh == 0:
+                full.extend(banks_of(c - 1))
+            before = pairs
+        multiply(c, gh, (0,), rq)
+        rq = ready(pairs, (1,))
         drain(len(full), False)
-        multiply(c, gh, 1, rq2)
+        multiply(c, gh, (1,), rq)
         for n, (j, half) in enumerate(banks_of(c)):
             store(j, half, n % 2 == 1)

@@ -20,10 +20,10 @@ ALU = mybir.AluOpType
 P = 128
 BANK = 512
 TILES = N // P
-CHUNKS = (128, 256, 256, 256, 128)
+CHUNKS = (256, 256, 256, 128, 128)
 LN_FLOOR = 2.0 ** -63
 VECTOR_WIDENS = (0, 2)
-WARM_HEAD = 5
+WARM_HEAD = 6
 WARM_EACH = 2
 DRAIN = 2
 
@@ -72,8 +72,8 @@ def tile_fractionaljacobikantwodegree_w4_kernel(
         warm_out = keep.tile([P, 1], F32)
         nc.scalar.activation(out=warm_out[:], in_=warm[:], func=ACT.Sigmoid)
         nc.sync.dma_start(out=xb[1][:], in_=x_rows[:, 2:4, :])
-        nc.sync.dma_start(out=w1_raw[:].bitcast(I32), in_=w1_words.rearrange("g p b -> p g b").bitcast(I32))
         nc.sync.dma_start(out=xb[2][:], in_=x_rows[:, 4:6, :])
+        nc.sync.dma_start(out=w1_raw[:].bitcast(I32), in_=w1_words.rearrange("g p b -> p g b").bitcast(I32))
         nc.sync.dma_start(out=xb[3][:], in_=x_rows[:, 6:8, :])
         for quad in range(4):
             nc.sync.dma_start(
@@ -125,19 +125,6 @@ def tile_fractionaljacobikantwodegree_w4_kernel(
                 op=ALU.mult,
             )
 
-        def scale_x_planes(q, gk):
-            planes = keep.tile([P, 4, 256], BF16)
-            turned = xt[q, gk][:].bitcast(BF16).rearrange("p (u n e) -> p u e n", u=2, e=2)
-            for t in range(4):
-                nc.scalar.activation(
-                    out=planes[:, t, :], in_=turned[:, t // 2, t % 2, :], func=ACT.Copy, scale=xsc[:, gk, t : t + 1]
-                )
-            return planes
-
-        def interleave_x(q, gk, planes):
-            xq[q, gk] = work.tile([P, 1024], BF16, name="xq", bufs=4, align_bytes=64)
-            interleave(xq[q, gk][:], planes[:])
-
         x_codes = [keep.tile([P, N], U32, name="xcodes%d" % gk, align_bytes=64) for gk in range(2)]
         x_scales = [keep.tile([P, N], U8, name="xscales%d" % gk, align_bytes=64) for gk in range(2)]
 
@@ -149,13 +136,13 @@ def tile_fractionaljacobikantwodegree_w4_kernel(
         w1s = keep.tile([P, 2, H], U8, align_bytes=64)
 
         def order_w1_codes():
-            nc.vector.tensor_copy(
+            nc.gpsimd.tensor_copy(
                 out=w1c[:].bitcast(I32).rearrange("p g (h t a e) -> p (g h) t a e", h=2, t=4, e=2),
                 in_=w1_raw[:].bitcast(I32).rearrange("p g (h a t e) -> p (g h) t a e", h=2, t=4, e=2),
             )
 
         def order_w1_scales():
-            nc.vector.tensor_copy(
+            nc.gpsimd.tensor_copy(
                 out=w1s[:].bitcast(I32).rearrange("p g (h t a) -> p (g h) t a", h=2, t=4),
                 in_=w1s_raw[:].bitcast(I32).rearrange("p g (h a t) -> p (g h) t a", h=2, t=4),
             )
@@ -187,6 +174,8 @@ def tile_fractionaljacobikantwodegree_w4_kernel(
                 nc.tensor.matmul(scratch[:], lhsT=idle[:, 0:P], rhs=idle[:], start=True, stop=True)
 
         warm_tensor(WARM_HEAD)
+        order_w1_codes()
+        order_w1_scales()
         for j in range(TILES):
             widen(j)
         turn(0)
@@ -194,24 +183,20 @@ def tile_fractionaljacobikantwodegree_w4_kernel(
         turn(1)
         warm_tensor(WARM_EACH)
         scale_x(0, 0)
-        order_w1_codes()
         scale_x(0, 1)
-        quantize_x(0, 0)
         turn(2)
         warm_tensor(WARM_EACH)
         scale_x(1, 0)
-        quantize_x(0, 1)
-        order_w1_scales()
         scale_x(1, 1)
         turn(3)
-        quantize_x(1, 0)
-        quantize_x(1, 1)
-        planes = scale_x_planes(2, 0)
+        for q in range(2):
+            for gk in range(2):
+                quantize_x(q, gk)
+        scale_x(2, 0)
         scale_x(2, 1)
-        interleave_x(2, 0, planes)
-        quantize_x(2, 1)
-        scale_x(3, 0)
         quantize_x(2, 0)
+        scale_x(3, 0)
+        quantize_x(2, 1)
         scale_x(3, 1)
         quantize_x(3, 0)
         quantize_x(3, 1)
@@ -330,21 +315,24 @@ def tile_fractionaljacobikantwodegree_w4_kernel(
                 scalar2=cst["k2"][:, t, gh : gh + 1], op0=ALU.mult, op1=ALU.add,
             )
 
+        def part_width(j):
+            return BANK // 2 if j == TILES - 1 else BANK
+
         def multiply(c, gh, degrees, rq):
             width = len(degrees) * CHUNKS[c]
-            codes = work.tile([P, width], U32, name="rcodes", align_bytes=64)
-            scales = work.tile([P, width], U8, name="rscales", align_bytes=64)
+            codes = work.tile([P, width], U32, name="rcodes", bufs=4, align_bytes=64)
+            scales = work.tile([P, width], U8, name="rscales", bufs=4, align_bytes=64)
             quantize(codes[:], scales[:], rq[:])
             for jj in range(CHUNKS[c] // P):
                 j = starts[c] // P + jj
-                for half in range(2):
-                    cols = slice(BANK * half, BANK * (half + 1))
+                for half in range(O // part_width(j)):
+                    cols = slice(part_width(j) * half, part_width(j) * (half + 1))
                     for n, d in enumerate(degrees):
                         if gh == 0 and d == 0:
-                            acc[j, half] = bank((2 * j + half) % 8)
+                            acc[j, half] = bank((2 * j + half) % 8)[:, 0 : part_width(j)]
                         toks = slice(CHUNKS[c] * n + P * jj, CHUNKS[c] * n + P * (jj + 1))
                         nc.tensor.matmul_mx(
-                            out=acc[j, half][:],
+                            out=acc[j, half],
                             lhsT=codes[:, toks].bitcast(FP8X4),
                             lhsT_scale=scales[:, toks],
                             rhs=w2_codes[d, gh][:, cols].bitcast(FP8X4),
@@ -354,15 +342,16 @@ def tile_fractionaljacobikantwodegree_w4_kernel(
                         )
 
         def store(j, half, on_vector):
-            y = work.tile([P, BANK], F32, name="y", bufs=8)
+            y = work.tile([P, part_width(j)], F32, name="y", bufs=8)
             if on_vector:
-                nc.vector.tensor_copy(out=y[:], in_=acc[j, half][:])
+                nc.vector.tensor_copy(out=y[:], in_=acc[j, half])
             else:
-                nc.scalar.copy(out=y[:], in_=acc[j, half][:])
-            nc.sync.dma_start(out=out_rows[:, j, BANK * half : BANK * (half + 1)], in_=y[:])
+                nc.scalar.copy(out=y[:], in_=acc[j, half])
+            nc.sync.dma_start(out=out_rows[:, j, part_width(j) * half : part_width(j) * (half + 1)], in_=y[:])
 
         def banks_of(c):
-            return [(starts[c] // P + jj, half) for jj in range(CHUNKS[c] // P) for half in range(2)]
+            tiles = range(starts[c] // P, (starts[c] + CHUNKS[c]) // P)
+            return [(j, half) for j in tiles for half in range(O // part_width(j))]
 
         def scalar_step(i):
             c, gh = steps[i]
@@ -400,15 +389,19 @@ def tile_fractionaljacobikantwodegree_w4_kernel(
             drain(DRAIN, False)
             pairs = work.tile([P, 2, 4, CHUNKS[c]], BF16, name="pairs")
             degree_one(pairs, c, gh, 0)
+            if i > 0:
+                rq = ready(before, (0,))
             degree_one(pairs, c, gh, 1)
-            if i > 0:
-                rq = ready(before, (0, 1))
             degree_two(pairs, c, gh, 0)
-            degree_one(pairs, c, gh, 2)
-            degree_two(pairs, c, gh, 1)
             if i > 0:
-                multiply(steps[i - 1][0], steps[i - 1][1], (0, 1), rq)
+                rq2 = ready(before, (1,))
+            degree_one(pairs, c, gh, 2)
+            if i > 0:
+                multiply(steps[i - 1][0], steps[i - 1][1], (0,), rq)
+            degree_two(pairs, c, gh, 1)
             degree_one(pairs, c, gh, 3)
+            if i > 0:
+                multiply(steps[i - 1][0], steps[i - 1][1], (1,), rq2)
             degree_two(pairs, c, gh, 2)
             if i == last:
                 rq = ready(pairs, (0,))

@@ -18,14 +18,21 @@ ACT = mybir.ActivationFunctionType
 ALU = mybir.AluOpType
 
 P = 128
+PACK = 4
 BANK = 512
+BANKS = 8
 TILES = N // P
+PAIR = 2 * P
+PASSES = 2
+DEGREES = 2
 CHUNKS = (256, 256, 256, 128, 128)
+TURN_BANKS = 5
 LN_FLOOR = 2.0 ** -63
 VECTOR_WIDENS = (0, 2)
 WARM_HEAD = 6
 WARM_EACH = 2
 DRAIN = 2
+VECTOR_SQUARES = 2
 
 
 def tile_fractionaljacobikantwodegree_w4_kernel(
@@ -39,143 +46,123 @@ def tile_fractionaljacobikantwodegree_w4_kernel(
         psum = ctx.enter_context(tc.psum_pool(name="psum", bufs=1))
         ctx.enter_context(tc.manual_schedule())
 
-        def bank(i):
-            return psum.tile([P, BANK], F32, name="bank%d" % i, tag="bank%d" % i)
+        def bank(n):
+            return psum.tile([P, BANK], F32, name="bank%d" % n, tag="bank%d" % n)
 
         def interleave(dst, src):
             nc.vector.tensor_copy(
-                out=dst.rearrange("p (c i t) -> p c t i", i=4, t=4),
+                out=dst.rearrange("p (c i t) -> p c t i", i=4, t=PACK),
                 in_=src.rearrange("p t (c i) -> p c t i", i=4),
             )
 
         def quantize(codes, scales, src):
             nc.vector.quantize_mx(out=codes.bitcast(FP8X4), scales=scales, in_=src)
 
-        warm = keep.tile([P, 1], F32)
-        nc.vector.memset(warm[:], 0.0)
-        w1s_raw = keep.tile([P, 2, H], U8)
-        nc.vector.memset(w1s_raw[:].bitcast(I32), 0)
-        idle = keep.tile([P, BANK], BF16)
-        nc.vector.memset(idle[:], 0.0)
+        zero = keep.tile([P, 1], F32)
+        nc.vector.memset(zero[:], 0.0)
+        w1_scales_raw = keep.tile([P, PASSES, H], U8)
+        nc.vector.memset(w1_scales_raw[:].bitcast(I32), 0)
+        warm_operand = keep.tile([P, BANK], BF16)
+        nc.vector.memset(warm_operand[:], 0.0)
         ident = keep.tile([P, P], F32)
         make_identity(nc, ident[:])
-        par_raw = keep.tile([P, BANK], BF16)
-        nc.gpsimd.memset(par_raw[:], 0.0)
+        par_rows = keep.tile([P, BANK], BF16)
+        nc.gpsimd.memset(par_rows[:], 0.0)
 
         x_rows = x_bytes.rearrange("(p j) k -> p j k", j=TILES)
-        xb = [keep.tile([P, 2, D], U8, name="xb%d" % q) for q in range(4)]
-        xsc = keep.tile([P, 2, 4], F32)
-        w1_raw = keep.tile([P, 2, 2 * H], U8)
-        nc.sync.dma_start(out=xb[0][:], in_=x_rows[:, 0:2, :])
-        with nc.allow_non_contiguous_dma(reason="small vectors"):
-            nc.scalar.dma_start(out=xsc[:], in_=x_scale.rearrange("o (g p t) -> p (o g) t", p=P, t=4))
-        warm_out = keep.tile([P, 1], F32)
-        nc.scalar.activation(out=warm_out[:], in_=warm[:], func=ACT.Sigmoid)
-        nc.sync.dma_start(out=xb[1][:], in_=x_rows[:, 2:4, :])
-        nc.sync.dma_start(out=xb[2][:], in_=x_rows[:, 4:6, :])
-        nc.sync.dma_start(out=w1_raw[:].bitcast(I32), in_=w1_words.rearrange("g p b -> p g b").bitcast(I32))
-        nc.sync.dma_start(out=xb[3][:], in_=x_rows[:, 6:8, :])
+        x_raw = [keep.tile([P, 2, D], U8, name="x_raw%d" % q) for q in range(TILES // 2)]
+
+        def load_x(q):
+            nc.sync.dma_start(out=x_raw[q][:], in_=x_rows[:, 2 * q : 2 * q + 2, :])
+
+        load_x(0)
+        k_scale = keep.tile([P, PASSES, PACK], F32)
+        with nc.allow_non_contiguous_dma(reason="four scales a partition and pass"):
+            nc.scalar.dma_start(out=k_scale[:], in_=x_scale.rearrange("o (kp p t) -> p (o kp) t", p=P, t=PACK))
+        warm_result = keep.tile([P, 1], F32)
+        nc.scalar.activation(out=warm_result[:], in_=zero[:], func=ACT.Sigmoid)
+        load_x(1)
+        load_x(2)
+        w1_raw = keep.tile([P, PASSES, 2 * H], U8)
+        nc.sync.dma_start(out=w1_raw[:].bitcast(I32), in_=w1_words.rearrange("kp p b -> p kp b").bitcast(I32))
+        load_x(3)
         for quad in range(4):
             nc.sync.dma_start(
-                out=w1s_raw[32 * quad : 32 * quad + 4, :, :].bitcast(I32),
-                in_=w1_scales[:, 4 * quad : 4 * quad + 4, :].rearrange("g r n -> r g n").bitcast(I32),
+                out=w1_scales_raw[32 * quad : 32 * quad + 4, :, :].bitcast(I32),
+                in_=w1_scales[:, 4 * quad : 4 * quad + 4, :].rearrange("kp r n -> r kp n").bitcast(I32),
             )
         w2_raw = {}
-        for gh in range(2):
-            for d in range(2):
-                w2_raw[d, gh] = keep.tile([P, 4, O], BF16, name="w2raw%d%d" % (d, gh))
-                rows = w2[d, 512 * gh : 512 * (gh + 1), :].rearrange("(a t e) n -> e a t n", t=4, e=4)
+        for hp in range(PASSES):
+            for d in range(DEGREES):
+                w2_raw[d, hp] = keep.tile([P, PACK, O], BF16, name="w2_raw%d%d" % (d, hp))
+                rows = w2[d, 512 * hp : 512 * (hp + 1), :].rearrange("(a t e) n -> e a t n", t=PACK, e=4)
                 for e in range(4):
-                    nc.sync.dma_start(out=w2_raw[d, gh][e:P:4, :, :], in_=rows[e])
-        for v, vec in enumerate((gamma, alpha, beta)):
-            nc.sync.dma_start(out=par_raw[2 * v : 2 * v + 2, :], in_=vec.rearrange("(h c) -> h c", h=2))
-        nc.sync.dma_start(out=par_raw[6:10, :], in_=g.rearrange("d (h c) -> (d h) c", h=2))
+                    nc.sync.dma_start(out=w2_raw[d, hp][e:P:4, :, :], in_=rows[e])
+        for n, vector in enumerate((gamma, alpha, beta)):
+            nc.sync.dma_start(out=par_rows[2 * n : 2 * n + 2, :], in_=vector.rearrange("(hp c) -> hp c", hp=PASSES))
+        nc.sync.dma_start(out=par_rows[6:10, :], in_=g.rearrange("d (hp c) -> (d hp) c", hp=PASSES))
 
-        xw = [keep.tile([P, D], BF16, name="xw%d" % j) for j in range(TILES)]
+        w1_codes = keep.tile([P, PASSES, 2 * H], U8, align_bytes=64)
+        w1_scale_plane = keep.tile([P, PASSES, H], U8, align_bytes=64)
+
+        def order_w1():
+            nc.gpsimd.tensor_copy(
+                out=w1_codes[:].bitcast(I32).rearrange("p kp (hp t a w) -> p (kp hp) t a w", hp=PASSES, t=PACK, w=2),
+                in_=w1_raw[:].bitcast(I32).rearrange("p kp (hp a t w) -> p (kp hp) t a w", hp=PASSES, t=PACK, w=2),
+            )
+            nc.gpsimd.tensor_copy(
+                out=w1_scale_plane[:].bitcast(I32).rearrange("p kp (hp t a) -> p (kp hp) t a", hp=PASSES, t=PACK),
+                in_=w1_scales_raw[:].bitcast(I32).rearrange("p kp (hp a t) -> p (kp hp) t a", hp=PASSES, t=PACK),
+            )
+
+        def warm_tensor(count):
+            scratch = bank(BANKS - 1)
+            for n in range(count):
+                nc.tensor.matmul(scratch[:], lhsT=warm_operand[:, 0:P], rhs=warm_operand[:], start=True, stop=True)
+
+        x_wide = [keep.tile([P, D], BF16, name="x_wide%d" % j) for j in range(TILES)]
 
         def widen(j):
-            src = xb[j // 2][:, j % 2, :].bitcast(FP8)
+            src = x_raw[j // 2][:, j % 2, :].bitcast(FP8)
             if j in VECTOR_WIDENS:
-                nc.vector.tensor_copy(out=xw[j][:], in_=src)
+                nc.vector.tensor_copy(out=x_wide[j][:], in_=src)
             else:
-                nc.scalar.copy(out=xw[j][:], in_=src)
+                nc.scalar.copy(out=x_wide[j][:], in_=src)
 
-        xt = {}
+        turned = {}
 
         def turn(q):
-            for gk in range(2):
-                xt[q, gk] = bank((2 * q + gk) % 5)
-            for gk in range(2):
+            for kp in range(PASSES):
+                turned[q, kp] = bank((PASSES * q + kp) % TURN_BANKS)
+            for kp in range(PASSES):
                 for jj in range(2):
-                    words = xw[2 * q + jj][:].bitcast(F32)
+                    words = x_wide[2 * q + jj][:].bitcast(F32)
                     for u in range(2):
-                        col = 256 * u + P * jj
+                        col = PAIR * u + P * jj
                         nc.tensor.transpose(
-                            xt[q, gk][:, col : col + P], words[:, 256 * gk + u : 256 * (gk + 1) : 2], ident[:]
+                            turned[q, kp][:, col : col + P], words[:, 256 * kp + u : 256 * (kp + 1) : 2], ident[:]
                         )
 
-        xq = {}
+        x_scaled = {}
 
-        def scale_x(q, gk):
-            xq[q, gk] = work.tile([P, 1024], BF16, name="xq", bufs=4, align_bytes=64)
+        def scale_x(q, kp):
+            x_scaled[q, kp] = work.tile([P, PACK * PAIR], BF16, name="x_scaled", bufs=4, align_bytes=64)
             nc.vector.tensor_tensor(
-                out=xq[q, gk][:].rearrange("p (n u e) -> p n u e", u=2, e=2),
-                in0=xt[q, gk][:].bitcast(BF16).rearrange("p (u n e) -> p n u e", u=2, e=2),
-                in1=xsc[:, gk, :].rearrange("p (u e) -> p u e", e=2).unsqueeze(1).to_broadcast([P, 256, 2, 2]),
+                out=x_scaled[q, kp][:].rearrange("p (n u b) -> p n u b", u=2, b=2),
+                in0=turned[q, kp][:].bitcast(BF16).rearrange("p (u n b) -> p n u b", u=2, b=2),
+                in1=k_scale[:, kp, :].rearrange("p (u b) -> p u b", b=2).unsqueeze(1).to_broadcast([P, PAIR, 2, 2]),
                 op=ALU.mult,
             )
 
-        x_codes = [keep.tile([P, N], U32, name="xcodes%d" % gk, align_bytes=64) for gk in range(2)]
-        x_scales = [keep.tile([P, N], U8, name="xscales%d" % gk, align_bytes=64) for gk in range(2)]
+        x_codes = [keep.tile([P, N], U32, name="x_codes%d" % kp, align_bytes=64) for kp in range(PASSES)]
+        x_scale_plane = [keep.tile([P, N], U8, name="x_plane%d" % kp, align_bytes=64) for kp in range(PASSES)]
 
-        def quantize_x(q, gk):
-            cols = slice(256 * q, 256 * (q + 1))
-            quantize(x_codes[gk][:, cols], x_scales[gk][:, cols], xq[q, gk][:])
-
-        w1c = keep.tile([P, 2, 2 * H], U8, align_bytes=64)
-        w1s = keep.tile([P, 2, H], U8, align_bytes=64)
-
-        def order_w1_codes():
-            nc.gpsimd.tensor_copy(
-                out=w1c[:].bitcast(I32).rearrange("p g (h t a e) -> p (g h) t a e", h=2, t=4, e=2),
-                in_=w1_raw[:].bitcast(I32).rearrange("p g (h a t e) -> p (g h) t a e", h=2, t=4, e=2),
-            )
-
-        def order_w1_scales():
-            nc.gpsimd.tensor_copy(
-                out=w1s[:].bitcast(I32).rearrange("p g (h t a) -> p (g h) t a", h=2, t=4),
-                in_=w1s_raw[:].bitcast(I32).rearrange("p g (h a t) -> p (g h) t a", h=2, t=4),
-            )
-
-        z = {}
-
-        def project(half, ht, gk):
-            if gk == 0:
-                z[half, ht] = bank(5 + (8 * half + ht) % 3)
-            cols = slice(BANK * half, BANK * (half + 1))
-            nc.tensor.matmul_mx(
-                out=z[half, ht][:],
-                lhsT=w1c[:, gk, 2 * P * ht : 2 * P * (ht + 1)].bitcast(FP4X4),
-                lhsT_scale=w1s[:, gk, P * ht : P * (ht + 1)],
-                rhs=x_codes[gk][:, cols].bitcast(FP8X4),
-                rhs_scale=x_scales[gk][:, cols],
-                start=(gk == 0),
-                stop=(gk == 1),
-            )
-
-        s = keep.tile([P, 8, N], F32)
-
-        def sigmoid(half, ht):
-            nc.scalar.activation(out=s[:, ht, BANK * half : BANK * (half + 1)], in_=z[half, ht][:], func=ACT.Sigmoid)
-
-        def warm_tensor(count):
-            scratch = bank(7)
-            for n in range(count):
-                nc.tensor.matmul(scratch[:], lhsT=idle[:, 0:P], rhs=idle[:], start=True, stop=True)
+        def quantize_x(q, kp):
+            cols = slice(PAIR * q, PAIR * (q + 1))
+            quantize(x_codes[kp][:, cols], x_scale_plane[kp][:, cols], x_scaled[q, kp][:])
 
         warm_tensor(WARM_HEAD)
-        order_w1_codes()
-        order_w1_scales()
+        order_w1()
         for j in range(TILES):
             widen(j)
         turn(0)
@@ -190,8 +177,8 @@ def tile_fractionaljacobikantwodegree_w4_kernel(
         scale_x(1, 1)
         turn(3)
         for q in range(2):
-            for gk in range(2):
-                quantize_x(q, gk)
+            for kp in range(PASSES):
+                quantize_x(q, kp)
         scale_x(2, 0)
         scale_x(2, 1)
         quantize_x(2, 0)
@@ -200,218 +187,256 @@ def tile_fractionaljacobikantwodegree_w4_kernel(
         scale_x(3, 1)
         quantize_x(3, 0)
         quantize_x(3, 1)
-        for half in range(2):
-            for ht in range(8):
-                for gk in range(2):
-                    project(half, ht, gk)
-                sigmoid(half, ht)
 
-        for pair in range(4):
-            both = s[:, 2 * pair : 2 * pair + 2, :]
-            nc.scalar.activation(out=both, in_=both, func=ACT.Ln, bias=LN_FLOOR)
+        log_sig = keep.tile([P, PASSES * PACK, N], F32)
+        for half in range(N // BANK):
+            tokens = slice(BANK * half, BANK * (half + 1))
+            for ht in range(PASSES * PACK):
+                z = bank(TURN_BANKS + (PASSES * PACK * half + ht) % (BANKS - TURN_BANKS))
+                for kp in range(PASSES):
+                    nc.tensor.matmul_mx(
+                        out=z[:],
+                        lhsT=w1_codes[:, kp, 2 * P * ht : 2 * P * (ht + 1)].bitcast(FP4X4),
+                        lhsT_scale=w1_scale_plane[:, kp, P * ht : P * (ht + 1)],
+                        rhs=x_codes[kp][:, tokens].bitcast(FP8X4),
+                        rhs_scale=x_scale_plane[kp][:, tokens],
+                        start=(kp == 0),
+                        stop=(kp == PASSES - 1),
+                    )
+                nc.scalar.activation(out=log_sig[:, ht, tokens], in_=z[:], func=ACT.Sigmoid)
+        for ht in range(0, PASSES * PACK, 2):
+            two_tiles = log_sig[:, ht : ht + 2, :]
+            nc.scalar.activation(out=two_tiles, in_=two_tiles, func=ACT.Ln, bias=LN_FLOOR)
 
-        par_f32 = keep.tile([P, BANK], F32)
-        par = keep.tile([P, 4, 16], F32)
-        cst = {name: keep.tile([P, 4, 2], F32, name=name) for name in
-               ("s4", "rec", "nb2", "h", "a1", "b1", "t1", "a2", "t2", "k2")}
-        ga, al, be, g0, g1 = [par[:, :, 2 * v : 2 * v + 2] for v in range(5)]
+        par_ordered = keep.tile([P, BANK], F32)
+        par = keep.tile([P, PACK, 16], F32)
+        gamma_c, alpha_c, beta_c, g0_c, g1_c = [par[:, :, 2 * n : 2 * n + 2] for n in range(5)]
+        names = ("s", "inv_s", "neg_b2", "shift", "lin1", "const1", "s_s1", "quad", "a2_shift", "vertex",
+                 "shift2", "half_b2_g1", "const2")
+        cst = {name: keep.tile([P, PACK, PASSES], F32, name=name) for name in names}
 
-        def stt(name, in0, scalar, in1, op0, op1):
-            nc.vector.scalar_tensor_tensor(out=cst[name][:], in0=in0, scalar=scalar, in1=in1, op0=op0, op1=op1)
+        def fused(name, in0, number, in1, op0):
+            nc.vector.scalar_tensor_tensor(out=cst[name][:], in0=in0, scalar=number, in1=in1, op0=op0, op1=ALU.mult)
 
-        def par_widen():
+        def order_par():
             nc.vector.tensor_copy(
-                out=par_f32[:].rearrange("p (t a e) -> p t a e", t=4, e=4),
-                in_=par_raw[:].rearrange("p (a t e) -> p t a e", t=4, e=4),
+                out=par_ordered[:].rearrange("r (t a e) -> r t a e", t=PACK, e=4),
+                in_=par_rows[:].rearrange("r (a t e) -> r t a e", t=PACK, e=4),
             )
 
-        def par_turn():
-            par_t = bank(0)
-            for t in range(4):
-                nc.tensor.transpose(par_t[:, P * t : P * (t + 1)], par_f32[:, P * t : P * (t + 1)], ident[:])
-            nc.vector.tensor_copy(out=par[:], in_=par_t[:].rearrange("p (t c) -> p t c", t=4)[:, :, 0:16])
+        def turn_par():
+            par_bank = bank(0)
+            for t in range(PACK):
+                cols = slice(P * t, P * (t + 1))
+                nc.tensor.transpose(par_bank[:, cols], par_ordered[:, cols], ident[:])
+            nc.vector.tensor_copy(out=par[:], in_=par_bank[:].rearrange("p (t r) -> p t r", t=PACK)[:, :, 0:16])
 
-        def par_first():
-            stt("s4", al, 4.0, be, ALU.add, ALU.add)
-            nc.vector.tensor_scalar(out=cst["nb2"][:], in0=be, scalar1=2.0, scalar2=-1.0, op0=ALU.add, op1=ALU.mult)
-            stt("b1", be, 1.0, g0, ALU.add, ALU.mult)
+        def constants_1():
+            nc.vector.scalar_tensor_tensor(
+                out=cst["s"][:], in0=alpha_c, scalar=4.0, in1=beta_c, op0=ALU.add, op1=ALU.add
+            )
+            nc.vector.tensor_scalar(
+                out=cst["neg_b2"][:], in0=beta_c, scalar1=2.0, scalar2=-1.0, op0=ALU.add, op1=ALU.mult
+            )
+            fused("const1", beta_c, 1.0, g0_c, ALU.add)
 
-        def par_second():
-            nc.vector.reciprocal(out=cst["rec"][:], in_=cst["s4"][:])
-            stt("a1", cst["s4"][:], -2.0, g0, ALU.add, ALU.mult)
-            stt("t1", cst["s4"][:], -1.0, cst["s4"][:], ALU.add, ALU.mult)
+        def constants_2():
+            nc.vector.reciprocal(out=cst["inv_s"][:], in_=cst["s"][:])
+            fused("lin1", cst["s"][:], -2.0, g0_c, ALU.add)
+            fused("s_s1", cst["s"][:], -1.0, cst["s"][:], ALU.add)
 
-        def par_third():
-            nc.vector.tensor_tensor(out=cst["h"][:], in0=cst["nb2"][:], in1=cst["rec"][:], op=ALU.mult)
-            stt("a2", cst["t1"][:], 0.5, g1, ALU.mult, ALU.mult)
+        def constants_3():
+            nc.vector.tensor_tensor(out=cst["shift"][:], in0=cst["neg_b2"][:], in1=cst["inv_s"][:], op=ALU.mult)
+            fused("quad", cst["s_s1"][:], 0.5, g1_c, ALU.mult)
 
-        def par_fourth():
-            stt("t2", al, 2.0, cst["h"][:], ALU.add, ALU.mult)
+        def constants_4():
+            fused("a2_shift", alpha_c, 2.0, cst["shift"][:], ALU.add)
+            fused("shift2", cst["neg_b2"][:], 2.0, cst["inv_s"][:], ALU.mult)
+            fused("half_b2_g1", cst["neg_b2"][:], -0.5, g1_c, ALU.mult)
 
-        def par_fifth():
-            stt("k2", cst["t2"][:], 0.5, g1, ALU.mult, ALU.mult)
+        def constants_5():
+            fused("vertex", cst["a2_shift"][:], 0.5, g1_c, ALU.mult)
+            fused("const2", beta_c, 1.0, cst["half_b2_g1"][:], ALU.add)
 
-        par_steps = [par_widen, par_turn, par_first, par_second, par_third, par_fourth, par_fifth]
+        par_steps = (order_par, turn_par, constants_1, constants_2, constants_3, constants_4, constants_5)
 
         w2_codes = {}
-        w2_scales = {}
-        for gh in range(2):
-            for d in range(2):
-                w2_codes[d, gh] = keep.tile([P, O], U32, name="w2codes%d%d" % (d, gh), align_bytes=64)
-                w2_scales[d, gh] = keep.tile([P, O], U8, name="w2scales%d%d" % (d, gh), align_bytes=64)
-        pieces = [(d, gh, half) for gh in range(2) for d in range(2) for half in range(2)]
-        w2q = {}
+        w2_scale_plane = {}
+        for hp in range(PASSES):
+            for d in range(DEGREES):
+                w2_codes[d, hp] = keep.tile([P, O], U32, name="w2_codes%d%d" % (d, hp), align_bytes=64)
+                w2_scale_plane[d, hp] = keep.tile([P, O], U8, name="w2_plane%d%d" % (d, hp), align_bytes=64)
+        pieces = [(d, hp, slice(c0, c0 + BANK)) for hp in range(PASSES) for d in range(DEGREES) for c0 in (0, BANK)]
+        w2_grouped = {}
 
-        def interleave_w2(i):
-            d, gh, half = pieces[i]
-            w2q[i] = work.tile([P, 4 * BANK], BF16, name="w2q", align_bytes=64)
-            interleave(w2q[i][:], w2_raw[d, gh][:, :, BANK * half : BANK * (half + 1)])
-
-        def quantize_w2(i):
-            d, gh, half = pieces[i]
-            cols = slice(BANK * half, BANK * (half + 1))
-            quantize(w2_codes[d, gh][:, cols], w2_scales[d, gh][:, cols], w2q[i][:])
+        def interleave_w2(n):
+            d, hp, cols = pieces[n]
+            w2_grouped[n] = work.tile([P, PACK * BANK], BF16, name="w2_grouped", align_bytes=64)
+            interleave(w2_grouped[n][:], w2_raw[d, hp][:, :, cols])
 
         interleave_w2(0)
-        for i in range(len(pieces)):
-            if i + 1 < len(pieces):
-                interleave_w2(i + 1)
-            if i > 0:
-                par_steps[i - 1]()
-            quantize_w2(i)
+        for n, (d, hp, cols) in enumerate(pieces):
+            if n + 1 < len(pieces):
+                interleave_w2(n + 1)
+            if n > 0:
+                par_steps[n - 1]()
+            quantize(w2_codes[d, hp][:, cols], w2_scale_plane[d, hp][:, cols], w2_grouped[n][:])
 
         out_rows = out.rearrange("(p j) o -> p j o", j=TILES)
         starts = [sum(CHUNKS[:c]) for c in range(len(CHUNKS))]
-        steps = [(c, gh) for c in range(len(CHUNKS)) for gh in range(2)]
-        vt = {}
-        qt = {}
+        steps = [(c, hp) for c in range(len(CHUNKS)) for hp in range(PASSES)]
+        last = len(steps) - 1
+        two_steps = 2 * PACK
+        power = {}
+        second = {}
         acc = {}
 
-        def power(c, gh, t):
-            vt[c, gh, t] = work.tile([P, CHUNKS[c]], F32, name="v", bufs=8)
+        def column(values, i, t):
+            hp = steps[i][1]
+            return values[:, t, hp : hp + 1]
+
+        def vector_squares(i, t):
+            return i == 0 and t < VECTOR_SQUARES
+
+        def exponential(i, t):
+            c, hp = steps[i]
+            power[i, t] = work.tile([P, CHUNKS[c]], F32, name="power", bufs=two_steps)
             nc.scalar.activation(
-                out=vt[c, gh, t][:], in_=s[:, 4 * gh + t, starts[c] : starts[c] + CHUNKS[c]],
-                func=ACT.Exp, scale=ga[:, t, gh : gh + 1],
+                out=power[i, t][:],
+                in_=log_sig[:, PACK * hp + t, starts[c] : starts[c] + CHUNKS[c]],
+                func=ACT.Exp,
+                scale=column(gamma_c, i, t),
             )
 
-        def square(c, gh, t):
-            qt[c, gh, t] = work.tile([P, CHUNKS[c]], F32, name="q", bufs=8)
-            nc.scalar.activation(
-                out=qt[c, gh, t][:], in_=vt[c, gh, t][:], func=ACT.Square, bias=cst["h"][:, t, gh : gh + 1]
-            )
+        def second_degree(i, t):
+            second[i, t] = work.tile([P, CHUNKS[steps[i][0]]], F32, name="second", bufs=two_steps)
+            if vector_squares(i, t):
+                nc.vector.scalar_tensor_tensor(
+                    out=second[i, t][:],
+                    in0=power[i, t][:],
+                    scalar=column(cst["shift2"], i, t),
+                    in1=power[i, t][:],
+                    op0=ALU.add,
+                    op1=ALU.mult,
+                )
+            else:
+                nc.scalar.activation(
+                    out=second[i, t][:], in_=power[i, t][:], func=ACT.Square, bias=column(cst["shift"], i, t)
+                )
 
-        def slot(pairs, d, t):
-            return pairs[:, d, t, :]
+        def scalar_step(i):
+            exponential(i, 0)
+            if i > 0:
+                second_degree(i - 1, PACK - 1)
+            for t in range(1, PACK):
+                exponential(i, t)
+                if not vector_squares(i, t - 1):
+                    second_degree(i, t - 1)
+            if i == last:
+                second_degree(i, PACK - 1)
 
-        def degree_one(pairs, c, gh, t):
+        def make_r1(r, i, t):
             nc.vector.tensor_scalar(
-                out=slot(pairs, 0, t), in0=vt[c, gh, t][:], scalar1=cst["a1"][:, t, gh : gh + 1],
-                scalar2=cst["b1"][:, t, gh : gh + 1], op0=ALU.mult, op1=ALU.subtract,
+                out=r[:, 0, t, :],
+                in0=power[i, t][:],
+                scalar1=column(cst["lin1"], i, t),
+                scalar2=column(cst["const1"], i, t),
+                op0=ALU.mult,
+                op1=ALU.subtract,
+            )
+            if vector_squares(i, t):
+                second_degree(i, t)
+
+        def make_r2(r, i, t):
+            nc.vector.tensor_scalar(
+                out=r[:, 1, t, :],
+                in0=second[i, t][:],
+                scalar1=column(cst["quad"], i, t),
+                scalar2=column(cst["const2" if vector_squares(i, t) else "vertex"], i, t),
+                op0=ALU.mult,
+                op1=ALU.add,
             )
 
-        def degree_two(pairs, c, gh, t):
-            nc.vector.tensor_scalar(
-                out=slot(pairs, 1, t), in0=qt[c, gh, t][:], scalar1=cst["a2"][:, t, gh : gh + 1],
-                scalar2=cst["k2"][:, t, gh : gh + 1], op0=ALU.mult, op1=ALU.add,
-            )
+        def group(r, d):
+            grouped = work.tile([P, PACK * r.shape[3]], BF16, name="r_grouped", align_bytes=64)
+            interleave(grouped[:], r[:, d, :, :])
+            return grouped
 
         def part_width(j):
             return BANK // 2 if j == TILES - 1 else BANK
 
-        def multiply(c, gh, degrees, rq):
-            width = len(degrees) * CHUNKS[c]
-            codes = work.tile([P, width], U32, name="rcodes", bufs=4, align_bytes=64)
-            scales = work.tile([P, width], U8, name="rscales", bufs=4, align_bytes=64)
-            quantize(codes[:], scales[:], rq[:])
-            for jj in range(CHUNKS[c] // P):
-                j = starts[c] // P + jj
-                for half in range(O // part_width(j)):
-                    cols = slice(part_width(j) * half, part_width(j) * (half + 1))
-                    for n, d in enumerate(degrees):
-                        if gh == 0 and d == 0:
-                            acc[j, half] = bank((2 * j + half) % 8)[:, 0 : part_width(j)]
-                        toks = slice(CHUNKS[c] * n + P * jj, CHUNKS[c] * n + P * (jj + 1))
-                        nc.tensor.matmul_mx(
-                            out=acc[j, half],
-                            lhsT=codes[:, toks].bitcast(FP8X4),
-                            lhsT_scale=scales[:, toks],
-                            rhs=w2_codes[d, gh][:, cols].bitcast(FP8X4),
-                            rhs_scale=w2_scales[d, gh][:, cols],
-                            start=(gh == 0 and d == 0),
-                            stop=(gh == 1 and d == 1),
-                        )
-
-        def store(j, half, on_vector):
-            y = work.tile([P, part_width(j)], F32, name="y", bufs=8)
-            if on_vector:
-                nc.vector.tensor_copy(out=y[:], in_=acc[j, half])
-            else:
-                nc.scalar.copy(out=y[:], in_=acc[j, half])
-            nc.sync.dma_start(out=out_rows[:, j, part_width(j) * half : part_width(j) * (half + 1)], in_=y[:])
-
-        def banks_of(c):
+        def parts_of(c):
             tiles = range(starts[c] // P, (starts[c] + CHUNKS[c]) // P)
-            return [(j, half) for j in tiles for half in range(O // part_width(j))]
+            return [(j, part) for j in tiles for part in range(O // part_width(j))]
 
-        def scalar_step(i):
-            c, gh = steps[i]
-            power(c, gh, 0)
-            if i > 0:
-                square(steps[i - 1][0], steps[i - 1][1], 3)
-            for t in range(1, 4):
-                power(c, gh, t)
-                square(c, gh, t - 1)
-            if i == len(steps) - 1:
-                square(c, gh, 3)
+        def multiply(i, d, grouped):
+            c, hp = steps[i]
+            codes = work.tile([P, CHUNKS[c]], U32, name="r_codes", bufs=2 * DEGREES, align_bytes=64)
+            plane = work.tile([P, CHUNKS[c]], U8, name="r_plane", bufs=2 * DEGREES, align_bytes=64)
+            quantize(codes[:], plane[:], grouped[:])
+            for j, part in parts_of(c):
+                first = hp == 0 and d == 0
+                if first:
+                    acc[j, part] = bank((2 * j + part) % BANKS)[:, 0 : part_width(j)]
+                tokens = slice(P * j - starts[c], P * (j + 1) - starts[c])
+                cols = slice(part_width(j) * part, part_width(j) * (part + 1))
+                nc.tensor.matmul_mx(
+                    out=acc[j, part],
+                    lhsT=codes[:, tokens].bitcast(FP8X4),
+                    lhsT_scale=plane[:, tokens],
+                    rhs=w2_codes[d, hp][:, cols].bitcast(FP8X4),
+                    rhs_scale=w2_scale_plane[d, hp][:, cols],
+                    start=first,
+                    stop=(hp == PASSES - 1 and d == DEGREES - 1),
+                )
 
-        def ready(pairs, degrees):
-            some = pairs[:, degrees[0] : degrees[-1] + 1, :, :]
-            rq = work.tile([P, 4 * len(degrees) * some.shape[3]], BF16, name="rq", align_bytes=64)
-            nc.vector.tensor_copy(
-                out=rq[:].rearrange("p (d c i t) -> p d c t i", d=len(degrees), i=4, t=4),
-                in_=some.rearrange("p d t (c i) -> p d c t i", i=4),
-            )
-            return rq
+        def store(j, part, on_vector):
+            y = work.tile([P, part_width(j)], F32, name="y", bufs=BANKS)
+            if on_vector:
+                nc.vector.tensor_copy(out=y[:], in_=acc[j, part])
+            else:
+                nc.scalar.copy(out=y[:], in_=acc[j, part])
+            nc.sync.dma_start(out=out_rows[:, j, part_width(j) * part : part_width(j) * (part + 1)], in_=y[:])
 
-        last = len(steps) - 1
-        full = []
+        finished = []
 
-        def drain(count, on_vector):
-            for j, half in full[:count]:
-                store(j, half, on_vector)
-                full.remove((j, half))
+        def drain(count):
+            for j, part in finished[:count]:
+                store(j, part, False)
+                finished.remove((j, part))
 
         scalar_step(0)
-        before = None
-        for i, (c, gh) in enumerate(steps):
+        r_before = None
+        for i, (c, hp) in enumerate(steps):
             if i < last:
                 scalar_step(i + 1)
-            drain(DRAIN, False)
-            pairs = work.tile([P, 2, 4, CHUNKS[c]], BF16, name="pairs")
-            degree_one(pairs, c, gh, 0)
+            drain(DRAIN)
+            r = work.tile([P, DEGREES, PACK, CHUNKS[c]], BF16, name="r")
+            make_r1(r, i, 0)
             if i > 0:
-                rq = ready(before, (0,))
-            degree_one(pairs, c, gh, 1)
-            degree_two(pairs, c, gh, 0)
+                grouped1 = group(r_before, 0)
+            make_r1(r, i, 1)
+            make_r2(r, i, 0)
             if i > 0:
-                rq2 = ready(before, (1,))
-            degree_one(pairs, c, gh, 2)
+                grouped2 = group(r_before, 1)
+            make_r1(r, i, 2)
             if i > 0:
-                multiply(steps[i - 1][0], steps[i - 1][1], (0,), rq)
-            degree_two(pairs, c, gh, 1)
-            degree_one(pairs, c, gh, 3)
+                multiply(i - 1, 0, grouped1)
+            make_r2(r, i, 1)
+            make_r1(r, i, 3)
             if i > 0:
-                multiply(steps[i - 1][0], steps[i - 1][1], (1,), rq2)
-            degree_two(pairs, c, gh, 2)
+                multiply(i - 1, 1, grouped2)
+            make_r2(r, i, 2)
             if i == last:
-                rq = ready(pairs, (0,))
-            degree_two(pairs, c, gh, 3)
-            if i > 0 and gh == 0:
-                full.extend(banks_of(c - 1))
-            before = pairs
-        multiply(c, gh, (0,), rq)
-        rq = ready(pairs, (1,))
-        drain(len(full), False)
-        multiply(c, gh, (1,), rq)
-        for n, (j, half) in enumerate(banks_of(c)):
-            store(j, half, n % 2 == 1)
+                grouped1 = group(r, 0)
+            make_r2(r, i, 3)
+            if c > 0 and hp == 0:
+                finished.extend(parts_of(c - 1))
+            r_before = r
+
+        multiply(last, 0, grouped1)
+        grouped2 = group(r, 1)
+        drain(len(finished))
+        multiply(last, 1, grouped2)
+        for n, (j, part) in enumerate(parts_of(len(CHUNKS) - 1)):
+            store(j, part, n % 2 == 1)

from contextlib import ExitStack

import concourse.mybir as mybir
from concourse.masks import make_identity

N, D, H, O = 1024, 1024, 1024, 1024
FLOPS = 2 * N * D * H + 2 * 2 * N * H * O

F32 = mybir.dt.float32
BF16 = mybir.dt.bfloat16
I32 = mybir.dt.int32
U32 = mybir.dt.uint32
U8 = mybir.dt.uint8
FP8 = mybir.dt.float8_e4m3fn
FP8X4 = mybir.dt.float8_e4m3fn_x4
FP4X4 = mybir.dt.float4_e2m1fn_x4
ACT = mybir.ActivationFunctionType
ALU = mybir.AluOpType

P = 128
PACK = 4
BANK = 512
BANKS = 8
TILES = N // P
PAIR = 2 * P
PASSES = 2
DEGREES = 2
CHUNKS = (256, 256, 256, 128, 128)
TURN_BANKS = 5
LN_FLOOR = 2.0 ** -63
VECTOR_WIDENS = (0, 2)
WARM_HEAD = 6
WARM_EACH = 2
DRAIN = 2
VECTOR_SQUARES = 2


def tile_fractionaljacobikantwodegree_w4_kernel(
    tc, x_bytes, x_scale, w1_words, w1_scales, gamma, alpha, beta, g, w2, out
):
    nc = tc.nc

    with ExitStack() as ctx:
        keep = ctx.enter_context(tc.tile_pool(name="keep", bufs=1))
        work = ctx.enter_context(tc.tile_pool(name="work", bufs=3))
        psum = ctx.enter_context(tc.psum_pool(name="psum", bufs=1))
        ctx.enter_context(tc.manual_schedule())

        def bank(n):
            return psum.tile([P, BANK], F32, name="bank%d" % n, tag="bank%d" % n)

        def interleave(dst, src):
            nc.vector.tensor_copy(
                out=dst.rearrange("p (c i t) -> p c t i", i=4, t=PACK),
                in_=src.rearrange("p t (c i) -> p c t i", i=4),
            )

        def quantize(codes, scales, src):
            nc.vector.quantize_mx(out=codes.bitcast(FP8X4), scales=scales, in_=src)

        zero = keep.tile([P, 1], F32)
        nc.vector.memset(zero[:], 0.0)
        w1_scales_raw = keep.tile([P, PASSES, H], U8)
        nc.vector.memset(w1_scales_raw[:].bitcast(I32), 0)
        warm_operand = keep.tile([P, BANK], BF16)
        nc.vector.memset(warm_operand[:], 0.0)
        ident = keep.tile([P, P], F32)
        make_identity(nc, ident[:])
        par_rows = keep.tile([P, BANK], BF16)
        nc.gpsimd.memset(par_rows[:], 0.0)

        x_rows = x_bytes.rearrange("(p j) k -> p j k", j=TILES)
        x_raw = [keep.tile([P, 2, D], U8, name="x_raw%d" % q) for q in range(TILES // 2)]

        def load_x(q):
            nc.sync.dma_start(out=x_raw[q][:], in_=x_rows[:, 2 * q : 2 * q + 2, :])

        load_x(0)
        k_scale = keep.tile([P, PASSES, PACK], F32)
        with nc.allow_non_contiguous_dma(reason="four scales a partition and pass"):
            nc.scalar.dma_start(out=k_scale[:], in_=x_scale.rearrange("o (kp p t) -> p (o kp) t", p=P, t=PACK))
        warm_result = keep.tile([P, 1], F32)
        nc.scalar.activation(out=warm_result[:], in_=zero[:], func=ACT.Sigmoid)
        load_x(1)
        load_x(2)
        w1_raw = keep.tile([P, PASSES, 2 * H], U8)
        nc.sync.dma_start(out=w1_raw[:].bitcast(I32), in_=w1_words.rearrange("kp p b -> p kp b").bitcast(I32))
        load_x(3)
        for quad in range(4):
            nc.sync.dma_start(
                out=w1_scales_raw[32 * quad : 32 * quad + 4, :, :].bitcast(I32),
                in_=w1_scales[:, 4 * quad : 4 * quad + 4, :].rearrange("kp r n -> r kp n").bitcast(I32),
            )
        w2_raw = {}
        for hp in range(PASSES):
            for d in range(DEGREES):
                w2_raw[d, hp] = keep.tile([P, PACK, O], BF16, name="w2_raw%d%d" % (d, hp))
                rows = w2[d, 512 * hp : 512 * (hp + 1), :].rearrange("(a t e) n -> e a t n", t=PACK, e=4)
                for e in range(4):
                    nc.sync.dma_start(out=w2_raw[d, hp][e:P:4, :, :], in_=rows[e])
        for n, vector in enumerate((gamma, alpha, beta)):
            nc.sync.dma_start(out=par_rows[2 * n : 2 * n + 2, :], in_=vector.rearrange("(hp c) -> hp c", hp=PASSES))
        nc.sync.dma_start(out=par_rows[6:10, :], in_=g.rearrange("d (hp c) -> (d hp) c", hp=PASSES))

        w1_codes = keep.tile([P, PASSES, 2 * H], U8, align_bytes=64)
        w1_scale_plane = keep.tile([P, PASSES, H], U8, align_bytes=64)

        def order_w1():
            nc.gpsimd.tensor_copy(
                out=w1_codes[:].bitcast(I32).rearrange("p kp (hp t a w) -> p (kp hp) t a w", hp=PASSES, t=PACK, w=2),
                in_=w1_raw[:].bitcast(I32).rearrange("p kp (hp a t w) -> p (kp hp) t a w", hp=PASSES, t=PACK, w=2),
            )
            nc.gpsimd.tensor_copy(
                out=w1_scale_plane[:].bitcast(I32).rearrange("p kp (hp t a) -> p (kp hp) t a", hp=PASSES, t=PACK),
                in_=w1_scales_raw[:].bitcast(I32).rearrange("p kp (hp a t) -> p (kp hp) t a", hp=PASSES, t=PACK),
            )

        def warm_tensor(count):
            scratch = bank(BANKS - 1)
            for n in range(count):
                nc.tensor.matmul(scratch[:], lhsT=warm_operand[:, 0:P], rhs=warm_operand[:], start=True, stop=True)

        x_wide = [keep.tile([P, D], BF16, name="x_wide%d" % j) for j in range(TILES)]

        def widen(j):
            src = x_raw[j // 2][:, j % 2, :].bitcast(FP8)
            if j in VECTOR_WIDENS:
                nc.vector.tensor_copy(out=x_wide[j][:], in_=src)
            else:
                nc.scalar.copy(out=x_wide[j][:], in_=src)

        turned = {}

        def turn(q):
            for kp in range(PASSES):
                turned[q, kp] = bank((PASSES * q + kp) % TURN_BANKS)
            for kp in range(PASSES):
                for jj in range(2):
                    words = x_wide[2 * q + jj][:].bitcast(F32)
                    for u in range(2):
                        col = PAIR * u + P * jj
                        nc.tensor.transpose(
                            turned[q, kp][:, col : col + P], words[:, 256 * kp + u : 256 * (kp + 1) : 2], ident[:]
                        )

        x_scaled = {}

        def scale_x(q, kp):
            x_scaled[q, kp] = work.tile([P, PACK * PAIR], BF16, name="x_scaled", bufs=4, align_bytes=64)
            nc.vector.tensor_tensor(
                out=x_scaled[q, kp][:].rearrange("p (n u b) -> p n u b", u=2, b=2),
                in0=turned[q, kp][:].bitcast(BF16).rearrange("p (u n b) -> p n u b", u=2, b=2),
                in1=k_scale[:, kp, :].rearrange("p (u b) -> p u b", b=2).unsqueeze(1).to_broadcast([P, PAIR, 2, 2]),
                op=ALU.mult,
            )

        x_codes = [keep.tile([P, N], U32, name="x_codes%d" % kp, align_bytes=64) for kp in range(PASSES)]
        x_scale_plane = [keep.tile([P, N], U8, name="x_plane%d" % kp, align_bytes=64) for kp in range(PASSES)]

        def quantize_x(q, kp):
            cols = slice(PAIR * q, PAIR * (q + 1))
            quantize(x_codes[kp][:, cols], x_scale_plane[kp][:, cols], x_scaled[q, kp][:])

        warm_tensor(WARM_HEAD)
        order_w1()
        for j in range(TILES):
            widen(j)
        turn(0)
        warm_tensor(WARM_EACH)
        turn(1)
        warm_tensor(WARM_EACH)
        scale_x(0, 0)
        scale_x(0, 1)
        turn(2)
        warm_tensor(WARM_EACH)
        scale_x(1, 0)
        scale_x(1, 1)
        turn(3)
        for q in range(2):
            for kp in range(PASSES):
                quantize_x(q, kp)
        scale_x(2, 0)
        scale_x(2, 1)
        quantize_x(2, 0)
        scale_x(3, 0)
        quantize_x(2, 1)
        scale_x(3, 1)
        quantize_x(3, 0)
        quantize_x(3, 1)

        log_sig = keep.tile([P, PASSES * PACK, N], F32)
        for half in range(N // BANK):
            tokens = slice(BANK * half, BANK * (half + 1))
            for ht in range(PASSES * PACK):
                z = bank(TURN_BANKS + (PASSES * PACK * half + ht) % (BANKS - TURN_BANKS))
                for kp in range(PASSES):
                    nc.tensor.matmul_mx(
                        out=z[:],
                        lhsT=w1_codes[:, kp, 2 * P * ht : 2 * P * (ht + 1)].bitcast(FP4X4),
                        lhsT_scale=w1_scale_plane[:, kp, P * ht : P * (ht + 1)],
                        rhs=x_codes[kp][:, tokens].bitcast(FP8X4),
                        rhs_scale=x_scale_plane[kp][:, tokens],
                        start=(kp == 0),
                        stop=(kp == PASSES - 1),
                    )
                nc.scalar.activation(out=log_sig[:, ht, tokens], in_=z[:], func=ACT.Sigmoid)
        for ht in range(0, PASSES * PACK, 2):
            two_tiles = log_sig[:, ht : ht + 2, :]
            nc.scalar.activation(out=two_tiles, in_=two_tiles, func=ACT.Ln, bias=LN_FLOOR)

        par_ordered = keep.tile([P, BANK], F32)
        par = keep.tile([P, PACK, 16], F32)
        gamma_c, alpha_c, beta_c, g0_c, g1_c = [par[:, :, 2 * n : 2 * n + 2] for n in range(5)]
        names = ("s", "inv_s", "neg_b2", "shift", "lin1", "const1", "s_s1", "quad", "a2_shift", "vertex",
                 "shift2", "half_b2_g1", "const2")
        cst = {name: keep.tile([P, PACK, PASSES], F32, name=name) for name in names}

        def fused(name, in0, number, in1, op0):
            nc.vector.scalar_tensor_tensor(out=cst[name][:], in0=in0, scalar=number, in1=in1, op0=op0, op1=ALU.mult)

        def order_par():
            nc.vector.tensor_copy(
                out=par_ordered[:].rearrange("r (t a e) -> r t a e", t=PACK, e=4),
                in_=par_rows[:].rearrange("r (a t e) -> r t a e", t=PACK, e=4),
            )

        def turn_par():
            par_bank = bank(0)
            for t in range(PACK):
                cols = slice(P * t, P * (t + 1))
                nc.tensor.transpose(par_bank[:, cols], par_ordered[:, cols], ident[:])
            nc.vector.tensor_copy(out=par[:], in_=par_bank[:].rearrange("p (t r) -> p t r", t=PACK)[:, :, 0:16])

        def constants_1():
            nc.vector.scalar_tensor_tensor(
                out=cst["s"][:], in0=alpha_c, scalar=4.0, in1=beta_c, op0=ALU.add, op1=ALU.add
            )
            nc.vector.tensor_scalar(
                out=cst["neg_b2"][:], in0=beta_c, scalar1=2.0, scalar2=-1.0, op0=ALU.add, op1=ALU.mult
            )
            fused("const1", beta_c, 1.0, g0_c, ALU.add)

        def constants_2():
            nc.vector.reciprocal(out=cst["inv_s"][:], in_=cst["s"][:])
            fused("lin1", cst["s"][:], -2.0, g0_c, ALU.add)
            fused("s_s1", cst["s"][:], -1.0, cst["s"][:], ALU.add)

        def constants_3():
            nc.vector.tensor_tensor(out=cst["shift"][:], in0=cst["neg_b2"][:], in1=cst["inv_s"][:], op=ALU.mult)
            fused("quad", cst["s_s1"][:], 0.5, g1_c, ALU.mult)

        def constants_4():
            fused("a2_shift", alpha_c, 2.0, cst["shift"][:], ALU.add)
            fused("shift2", cst["neg_b2"][:], 2.0, cst["inv_s"][:], ALU.mult)
            fused("half_b2_g1", cst["neg_b2"][:], -0.5, g1_c, ALU.mult)

        def constants_5():
            fused("vertex", cst["a2_shift"][:], 0.5, g1_c, ALU.mult)
            fused("const2", beta_c, 1.0, cst["half_b2_g1"][:], ALU.add)

        par_steps = (order_par, turn_par, constants_1, constants_2, constants_3, constants_4, constants_5)

        w2_codes = {}
        w2_scale_plane = {}
        for hp in range(PASSES):
            for d in range(DEGREES):
                w2_codes[d, hp] = keep.tile([P, O], U32, name="w2_codes%d%d" % (d, hp), align_bytes=64)
                w2_scale_plane[d, hp] = keep.tile([P, O], U8, name="w2_plane%d%d" % (d, hp), align_bytes=64)
        pieces = [(d, hp, slice(c0, c0 + BANK)) for hp in range(PASSES) for d in range(DEGREES) for c0 in (0, BANK)]
        w2_grouped = {}

        def interleave_w2(n):
            d, hp, cols = pieces[n]
            w2_grouped[n] = work.tile([P, PACK * BANK], BF16, name="w2_grouped", align_bytes=64)
            interleave(w2_grouped[n][:], w2_raw[d, hp][:, :, cols])

        interleave_w2(0)
        for n, (d, hp, cols) in enumerate(pieces):
            if n + 1 < len(pieces):
                interleave_w2(n + 1)
            if n > 0:
                par_steps[n - 1]()
            quantize(w2_codes[d, hp][:, cols], w2_scale_plane[d, hp][:, cols], w2_grouped[n][:])

        out_rows = out.rearrange("(p j) o -> p j o", j=TILES)
        starts = [sum(CHUNKS[:c]) for c in range(len(CHUNKS))]
        steps = [(c, hp) for c in range(len(CHUNKS)) for hp in range(PASSES)]
        last = len(steps) - 1
        two_steps = 2 * PACK
        power = {}
        second = {}
        acc = {}

        def column(values, i, t):
            hp = steps[i][1]
            return values[:, t, hp : hp + 1]

        def vector_squares(i, t):
            return i == 0 and t < VECTOR_SQUARES

        def exponential(i, t):
            c, hp = steps[i]
            power[i, t] = work.tile([P, CHUNKS[c]], F32, name="power", bufs=two_steps)
            nc.scalar.activation(
                out=power[i, t][:],
                in_=log_sig[:, PACK * hp + t, starts[c] : starts[c] + CHUNKS[c]],
                func=ACT.Exp,
                scale=column(gamma_c, i, t),
            )

        def second_degree(i, t):
            second[i, t] = work.tile([P, CHUNKS[steps[i][0]]], F32, name="second", bufs=two_steps)
            if vector_squares(i, t):
                nc.vector.scalar_tensor_tensor(
                    out=second[i, t][:],
                    in0=power[i, t][:],
                    scalar=column(cst["shift2"], i, t),
                    in1=power[i, t][:],
                    op0=ALU.add,
                    op1=ALU.mult,
                )
            else:
                nc.scalar.activation(
                    out=second[i, t][:], in_=power[i, t][:], func=ACT.Square, bias=column(cst["shift"], i, t)
                )

        def scalar_step(i):
            exponential(i, 0)
            if i > 0:
                second_degree(i - 1, PACK - 1)
            for t in range(1, PACK):
                exponential(i, t)
                if not vector_squares(i, t - 1):
                    second_degree(i, t - 1)
            if i == last:
                second_degree(i, PACK - 1)

        def make_r1(r, i, t):
            nc.vector.tensor_scalar(
                out=r[:, 0, t, :],
                in0=power[i, t][:],
                scalar1=column(cst["lin1"], i, t),
                scalar2=column(cst["const1"], i, t),
                op0=ALU.mult,
                op1=ALU.subtract,
            )
            if vector_squares(i, t):
                second_degree(i, t)

        def make_r2(r, i, t):
            nc.vector.tensor_scalar(
                out=r[:, 1, t, :],
                in0=second[i, t][:],
                scalar1=column(cst["quad"], i, t),
                scalar2=column(cst["const2" if vector_squares(i, t) else "vertex"], i, t),
                op0=ALU.mult,
                op1=ALU.add,
            )

        def group(r, d):
            grouped = work.tile([P, PACK * r.shape[3]], BF16, name="r_grouped", align_bytes=64)
            interleave(grouped[:], r[:, d, :, :])
            return grouped

        def part_width(j):
            return BANK // 2 if j == TILES - 1 else BANK

        def parts_of(c):
            tiles = range(starts[c] // P, (starts[c] + CHUNKS[c]) // P)
            return [(j, part) for j in tiles for part in range(O // part_width(j))]

        def multiply(i, d, grouped):
            c, hp = steps[i]
            codes = work.tile([P, CHUNKS[c]], U32, name="r_codes", bufs=2 * DEGREES, align_bytes=64)
            plane = work.tile([P, CHUNKS[c]], U8, name="r_plane", bufs=2 * DEGREES, align_bytes=64)
            quantize(codes[:], plane[:], grouped[:])
            for j, part in parts_of(c):
                first = hp == 0 and d == 0
                if first:
                    acc[j, part] = bank((2 * j + part) % BANKS)[:, 0 : part_width(j)]
                tokens = slice(P * j - starts[c], P * (j + 1) - starts[c])
                cols = slice(part_width(j) * part, part_width(j) * (part + 1))
                nc.tensor.matmul_mx(
                    out=acc[j, part],
                    lhsT=codes[:, tokens].bitcast(FP8X4),
                    lhsT_scale=plane[:, tokens],
                    rhs=w2_codes[d, hp][:, cols].bitcast(FP8X4),
                    rhs_scale=w2_scale_plane[d, hp][:, cols],
                    start=first,
                    stop=(hp == PASSES - 1 and d == DEGREES - 1),
                )

        def store(j, part, on_vector):
            y = work.tile([P, part_width(j)], F32, name="y", bufs=BANKS)
            if on_vector:
                nc.vector.tensor_copy(out=y[:], in_=acc[j, part])
            else:
                nc.scalar.copy(out=y[:], in_=acc[j, part])
            nc.sync.dma_start(out=out_rows[:, j, part_width(j) * part : part_width(j) * (part + 1)], in_=y[:])

        finished = []

        def drain(count):
            for j, part in finished[:count]:
                store(j, part, False)
                finished.remove((j, part))

        scalar_step(0)
        r_before = None
        for i, (c, hp) in enumerate(steps):
            if i < last:
                scalar_step(i + 1)
            drain(DRAIN)
            r = work.tile([P, DEGREES, PACK, CHUNKS[c]], BF16, name="r")
            make_r1(r, i, 0)
            if i > 0:
                grouped1 = group(r_before, 0)
            make_r1(r, i, 1)
            make_r2(r, i, 0)
            if i > 0:
                grouped2 = group(r_before, 1)
            make_r1(r, i, 2)
            if i > 0:
                multiply(i - 1, 0, grouped1)
            make_r2(r, i, 1)
            make_r1(r, i, 3)
            if i > 0:
                multiply(i - 1, 1, grouped2)
            make_r2(r, i, 2)
            if i == last:
                grouped1 = group(r, 0)
            make_r2(r, i, 3)
            if c > 0 and hp == 0:
                finished.extend(parts_of(c - 1))
            r_before = r

        multiply(last, 0, grouped1)
        grouped2 = group(r, 1)
        drain(len(finished))
        multiply(last, 1, grouped2)
        for n, (j, part) in enumerate(parts_of(len(CHUNKS) - 1)):
            store(j, part, n % 2 == 1)
